import numpy as np
import ml_dtypes


def mxq(x, axis, fmt="e4m3"):
    dtype, down = {"e4m3": (ml_dtypes.float8_e4m3fn, 7), "e5m2": (ml_dtypes.float8_e5m2, 14)}[fmt]
    v = np.moveaxis(np.asarray(x, np.float32).astype(ml_dtypes.bfloat16).astype(np.float64), axis, -1)
    blocks = v.reshape(v.shape[:-1] + (-1, 32))
    amax = np.abs(blocks).max(-1, keepdims=True)
    byte = np.maximum(np.where(amax > 0, np.frexp(amax)[1] - 1 + 127, 0) - down, 1)
    scale = np.exp2(byte - 127.0)
    codes = (blocks / scale).astype(np.float32).astype(dtype).astype(np.float64)
    return np.moveaxis((codes * scale).reshape(v.shape), -1, axis)


WIDE = False


def mx_kscale(k):
    if not WIDE:
        return np.ones(k)
    levels = np.array([10, -10, 5, -5, 0])
    if k % 512:
        return np.exp2(np.random.permutation(np.resize(levels, k // 32))).repeat(32)
    a = np.empty((k // 512, 16))
    for p in range(k // 512):
        a[p, :8] = np.random.permutation(np.resize(levels, 8))
        for g in range(8):
            far = levels[np.abs(levels - a[p, g]) >= 10]
            a[p, g + 8] = far[np.random.randint(len(far))]
    return np.exp2(a.ravel()).repeat(32)


def f64(x):
    return np.asarray(x).astype(np.float64)


def striped(idx):
    return np.tile(idx.reshape(-1, 16).T, (8, 1)).astype(np.uint16)


def unstriped(offs):
    return offs[:16].T.reshape(-1).astype(np.int64)


E2M1 = np.array([0.0, 0.5, 1.0, 1.5, 2.0, 3.0, 4.0, 6.0, -0.0, -0.5, -1.0, -1.5, -2.0, -3.0, -4.0, -6.0])


def pack_weight(w, fmt):
    k, n = w.shape
    w = f64(np.asarray(w, np.float32).astype(ml_dtypes.bfloat16)).reshape(k // 32, 32, n)
    amax = np.abs(w).max(1)
    if fmt == "e4m3":
        byte = np.frexp(amax)[1] - 1 + 127 - 7
    else:
        mant, ex = np.frexp(amax / 6.0)
        byte = np.where(mant > 0.5, ex, ex - 1) + 127
    byte = np.clip(np.where(amax > 0, byte, 1), 1, 254)
    scaled = (w * np.exp2(127.0 - byte)[:, None, :]).reshape(k, n).astype(np.float32)
    by_word = np.ascontiguousarray(scaled.reshape(k // 512, 128, 4, n).transpose(0, 1, 3, 2))
    if fmt == "e4m3":
        words = by_word.astype(ml_dtypes.float8_e4m3fn).view(np.uint8)
    else:
        c = by_word.astype(ml_dtypes.float4_e2m1fn).view(np.uint8) & 0xF
        words = (c[..., 0::2] | (c[..., 1::2] << 4)).reshape(k // 512, 128, 2 * n)
    return np.ascontiguousarray(words), np.ascontiguousarray(byte.astype(np.uint8).reshape(k // 512, 16, n))


def unpack_weight(words, scales, fmt):
    g, _, n = scales.shape
    words = np.ascontiguousarray(words).reshape(g, 128, n, -1)
    if fmt == "e4m3":
        vals = words.view(ml_dtypes.float8_e4m3fn).astype(np.float64)
    else:
        nib = np.empty((g, 128, n, 4), np.uint8)
        nib[..., 0::2] = words & 0xF
        nib[..., 1::2] = words >> 4
        vals = E2M1[nib]
    vals = vals * np.repeat(np.exp2(scales.astype(np.float64) - 127.0), 8, axis=1)[..., None]
    return vals.transpose(0, 1, 3, 2).reshape(g * 512, n)


K, T, G, C1, E, C2, H = 1024, 768, 3, 256, 6, 128, 512
N = 256


def by_expert(wq, xq, E, C):
    return np.concatenate([wq[e].T @ xq[:, e * C:(e + 1) * C] for e in range(E)], axis=1)


def setup_inputs():
    n = np.random.standard_normal
    s = mx_kscale(K)
    u = mx_kscale(H)
    slots1 = np.random.permutation(T)
    slots2 = np.concatenate([q * C1 + np.random.permutation(C1) for q in range(G)])
    x = pack_weight(n((K, T)) * s[:, None], "e4m3")
    wg = [pack_weight(m, "e2m1") for m in n((G, K, H)) / np.sqrt(K) / s[None, :, None] * u]
    we = [pack_weight(m, "e4m3") for m in n((E, H, N)) / np.sqrt(H) / u[None, :, None]]
    return {
        "x_words": x[0],
        "x_scales": x[1],
        "wg_words": np.stack([m[0] for m in wg]),
        "wg_scales": np.stack([m[1] for m in wg]),
        "we_words": np.stack([m[0] for m in we]),
        "we_scales": np.stack([m[1] for m in we]),
        "gate": (np.tile(np.random.uniform(0.2, 1.0, T), (128, 1))).astype(np.float32),
        "offs": striped(slots1),
        "offs2": striped(slots2),
        "dst": striped(slots1[slots2]),
    }


def reference(x_words, x_scales, wg_words, wg_scales, we_words, we_scales, gate, offs, offs2, dst):
    wg = np.stack([unpack_weight(wg_words[e], wg_scales[e], "e2m1") for e in range(G)])
    we = np.stack([unpack_weight(we_words[e], we_scales[e], "e4m3") for e in range(E)])
    idx, idx2 = unstriped(offs), unstriped(offs2)
    xq = unpack_weight(x_words, x_scales, "e4m3")[:, idx]
    a = by_expert(wg, xq, G, C1)
    y = by_expert(we, mxq(a[:, idx2], 0, "e4m3"), E, C2)
    out = np.zeros((N, T))
    out[:, unstriped(dst)] = f64(gate[:1]) * y
    return out

@@ -1,0 +1,186 @@
+from contextlib import ExitStack
+
+import concourse.mybir as mybir
+from concourse.masks import make_identity
+
+K, T, G, C1, E, C2, H, N = 1024, 768, 3, 256, 6, 128, 512, 256
+FLOPS = 2 * T * (K * H + H * N)
+
+F32 = mybir.dt.float32
+BF16 = mybir.dt.bfloat16
+I32 = mybir.dt.int32
+U32 = mybir.dt.uint32
+U16 = mybir.dt.uint16
+U8 = mybir.dt.uint8
+FP8X4 = mybir.dt.float8_e4m3fn_x4
+FP4X4 = mybir.dt.float4_e2m1fn_x4
+
+P = 128
+S = K // 512
+LC = C1 // 16
+FIRST_BLOCK = (0, 3, 5)
+PAD_BLOCK = 2
+BLOCKS = 7
+
+
+def tile_moe_hie_none_kernel(
+    tc, x_words, x_scales, wg_words, wg_scales, we_words, we_scales, gate, offs, offs2, dst, out
+):
+    nc = tc.nc
+    mult = mybir.AluOpType.mult
+
+    with ExitStack() as ctx:
+        keep = ctx.enter_context(tc.tile_pool(name="keep", bufs=1))
+        ps_a = ctx.enter_context(tc.psum_pool(name="ps_a", bufs=3))
+        ps_t = ctx.enter_context(tc.psum_pool(name="ps_t", bufs=2))
+        ps_y = ctx.enter_context(tc.psum_pool(name="ps_y", bufs=3))
+
+        def kept(shape, dtype, name):
+            return keep.tile(shape, dtype, name=name, align_bytes=64)
+
+        offs_sb = kept([P, T // 16], U16, "offs_sb")
+        offs2_sb = kept([P, T // 16], U16, "offs2_sb")
+        dst_sb = kept([P, T // 16], U16, "dst_sb")
+        xw = [kept([P, T], U32, "xw%d" % s) for s in range(S)]
+        xs = kept([P, S, T], U8, "xs")
+        wgw = [kept([P, S, 2 * H], U8, "wgw%d" % f) for f in range(G)]
+        wgs0 = kept([P, S, H], U8, "wgs0")
+        wgs12 = kept([P, 2 * S, H], U8, "wgs12")
+        wew = [kept([P, 2, N], U32, "wew%d" % f) for f in range(G)]
+        wes = kept([P, E, N], U8, "wes")
+        gate_sb = kept([P, T], F32, "gate_sb")
+        ident = kept([P, P], F32, "ident")
+        zeros = kept([P, C1], F32, "zeros")
+        pairs = kept([P, BLOCKS * 2 * C1], BF16, "pairs")
+        res = [kept([P, T], F32, "res%d" % h) for h in range(2)]
+
+        nc.vector.memset(xs[:].rearrange("p s t -> p (s t)").bitcast(I32), 0)
+        nc.vector.memset(wgs0[:].rearrange("p s t -> p (s t)").bitcast(I32), 0)
+        nc.vector.memset(wgs12[:].rearrange("p s t -> p (s t)").bitcast(I32), 0)
+        nc.gpsimd.memset(zeros[:], 0.0)
+        make_identity(nc, ident[:])
+        nc.gpsimd.memset(wes[:].rearrange("p s t -> p (s t)").bitcast(I32), 0)
+        pair_f32 = pairs[:].bitcast(F32)
+        pair_u32 = pairs[:].bitcast(U32)
+        nc.scalar.copy(pair_f32[:, PAD_BLOCK * C1:(PAD_BLOCK + 1) * C1], zeros[:])
+
+        def load_scales(plane, rows):
+            for q in range(4):
+                nc.sync.dma_start(
+                    plane[32 * q:32 * q + 4, :, :].bitcast(I32),
+                    rows[:, 4 * q:4 * q + 4, :].rearrange("c r w -> r c w").bitcast(I32),
+                )
+
+        def load_x(s):
+            nc.sync.dma_start(xw[s][:].bitcast(I32), x_words[s].rearrange("p t d -> p (t d)").bitcast(I32))
+
+        def load_wg(f):
+            nc.sync.dma_start(wgw[f][:].bitcast(I32), wg_words[f].rearrange("s p w -> p s w").bitcast(I32))
+
+        def load_we(f):
+            nc.sync.dma_start(
+                wew[f][:].bitcast(I32),
+                we_words[2 * f:2 * f + 2, 0].rearrange("e p n d -> p e (n d)").bitcast(I32),
+            )
+
+        nc.sync.dma_start(offs_sb[:], offs)
+        load_x(0)
+        load_scales(xs, x_scales)
+        load_x(1)
+        load_wg(0)
+        load_scales(wgs0, wg_scales[0])
+        load_wg(1)
+        load_scales(wgs12, wg_scales[1:3].rearrange("f s b i -> (f s) b i"))
+        nc.sync.dma_start(offs2_sb[:], offs2)
+        load_wg(2)
+        load_we(0)
+        load_scales(wes, we_scales.rearrange("e s b n -> (e s) b n"))
+        nc.sync.dma_start(dst_sb[:], dst)
+        nc.sync.dma_start(gate_sb[:], gate)
+        load_we(1)
+        load_we(2)
+
+        def group_layer(f):
+            cols = offs_sb[:, f * LC:(f + 1) * LC]
+            words = kept([P, S, C1], U32, "gw%d" % f)
+            scales = kept([P, S, C1], U8, "gs%d" % f)
+            for s in range(S):
+                nc.vector.tensor_copy(words[:, s, :], xw[s][:].indirect(cols))
+                nc.vector.tensor_copy(scales[:, s, :], xs[:, s, :].indirect(cols))
+            banks = [ps_a.tile([P, H], F32, name="a_bank") for b in range(2)]
+            for s in range(S):
+                w_scale = wgs0[:, s, :] if f == 0 else wgs12[:, (f - 1) * S + s, :]
+                for b in range(2):
+                    nc.tensor.matmul_mx(
+                        out=banks[b][:],
+                        lhsT=words[:, s, b * P:(b + 1) * P].bitcast(FP8X4),
+                        lhsT_scale=scales[:, s, b * P:(b + 1) * P],
+                        rhs=wgw[f][:, s, :].bitcast(FP4X4),
+                        rhs_scale=w_scale,
+                        start=(s == 0),
+                        stop=(s == S - 1),
+                    )
+            rounded = []
+            for b in range(2):
+                a_t = kept([P, H], BF16, "aT%d_%d" % (f, b))
+                nc.scalar.copy(
+                    a_t[:].rearrange("m (u p e) -> m u p e", u=2, e=2),
+                    banks[b][:].rearrange("m (p u e) -> m u p e", u=2, e=2),
+                )
+                rounded.append(a_t)
+            home = pair_f32[:, FIRST_BLOCK[f] * C1:(FIRST_BLOCK[f] + 2) * C1].rearrange("p (u j) -> p u j", u=2)
+            for b in range(2):
+                turned = ps_t.tile([P, 2, P], F32, name="turned")
+                for u in range(2):
+                    nc.tensor.transpose(turned[:, u, :], rounded[b][:].bitcast(F32)[:, u * P:(u + 1) * P], ident[:])
+                nc.scalar.copy(home[:, :, b * P:(b + 1) * P], turned[:])
+
+        def expert_layer(f):
+            cols = offs2_sb[:, f * LC:(f + 1) * LC]
+            picked = kept([P, 4 * C1], BF16, "picked%d" % f)
+            picked_u32 = picked[:].bitcast(U32).rearrange("p (m u) -> p m u", u=2)
+            for u in range(2):
+                first = (FIRST_BLOCK[f] + u - f) * C1
+                width = max(2, f + 1) * C1
+                nc.vector.tensor_copy(picked_u32[:, :, u], pair_u32[:, first:first + width].indirect(cols))
+            codes = kept([P, C1], U32, "codes%d" % f)
+            scales = kept([P, C1], U8, "ascale%d" % f)
+            nc.vector.quantize_mx(out=codes[:].bitcast(FP8X4), scales=scales[:], in_=picked[:])
+            ys = []
+            for h in range(2):
+                bank = ps_y.tile([P, C1], F32, name="y_bank")
+                for e in range(2):
+                    nc.tensor.matmul_mx(
+                        out=bank[:, e * C2:(e + 1) * C2],
+                        lhsT=wew[f][:, e, h * P:(h + 1) * P].bitcast(FP8X4),
+                        lhsT_scale=wes[:, 2 * f + e, h * P:(h + 1) * P],
+                        rhs=codes[:, e * C2:(e + 1) * C2].bitcast(FP8X4),
+                        rhs_scale=scales[:, e * C2:(e + 1) * C2],
+                        start=True,
+                        stop=True,
+                    )
+                y = kept([P, C1], F32, "y%d_%d" % (f, h))
+                nc.scalar.copy(y[:], bank[:])
+                ys.append(y)
+            return ys
+
+        def send_home(f, ys):
+            for h in range(2):
+                nc.vector.tensor_tensor(
+                    res[h][:].indirect(dst_sb[:, f * LC:(f + 1) * LC]),
+                    ys[h][:],
+                    gate_sb[:, f * C1:(f + 1) * C1],
+                    mult,
+                )
+
+        group_layer(0)
+        group_layer(1)
+        y0 = expert_layer(0)
+        group_layer(2)
+        y1 = expert_layer(1)
+        send_home(0, y0)
+        y2 = expert_layer(2)
+        send_home(1, y1)
+        send_home(2, y2)
+        for h in range(2):
+            nc.sync.dma_start(out[h * P:(h + 1) * P, :], res[h][:])

@@ -42,11 +42,14 @@ def tile_moe_hie_none_kernel(
         offs2_sb = kept([P, T // 16], U16, "offs2_sb")
         dst_sb = kept([P, T // 16], U16, "dst_sb")
         xw = [kept([P, T], U32, "xw%d" % s) for s in range(S)]
-        xs = kept([P, S, T], U8, "xs")
-        wgw = [kept([P, S, 2 * H], U8, "wgw%d" % f) for f in range(G)]
-        wgs0 = kept([P, S, H], U8, "wgs0")
-        wgs12 = kept([P, 2 * S, H], U8, "wgs12")
-        wew = [kept([P, 2, N], U32, "wew%d" % f) for f in range(G)]
+        xs = kept([P, T], U8, "xs")
+        wgw0 = kept([P, S, 2 * H], U8, "wgw0")
+        wgw12 = kept([P, 2 * S, 2 * H], U8, "wgw12")
+        wgs = kept([P, G * S, H], U8, "wgs")
+        wew = kept([P, E, N], U32, "wew")
+        spans = ((0, C1), (C1, T))
+        both = [kept([P, hi - lo], U8, "both%d" % lo) for lo, hi in spans]
+        second = [kept([P, hi - lo], U8, "second%d" % lo) for lo, hi in spans]
         wes = kept([P, E, N], U8, "wes")
         gate_sb = kept([P, T], F32, "gate_sb")
         ident = kept([P, P], F32, "ident")
@@ -54,12 +57,13 @@ def tile_moe_hie_none_kernel(
         pairs = kept([P, BLOCKS * 2 * C1], BF16, "pairs")
         res = [kept([P, T], F32, "res%d" % h) for h in range(2)]
 
-        nc.vector.memset(xs[:].rearrange("p s t -> p (s t)").bitcast(I32), 0)
-        nc.vector.memset(wgs0[:].rearrange("p s t -> p (s t)").bitcast(I32), 0)
-        nc.vector.memset(wgs12[:].rearrange("p s t -> p (s t)").bitcast(I32), 0)
+        nc.gpsimd.memset(xs[:].bitcast(I32), 0)
         nc.gpsimd.memset(zeros[:], 0.0)
+        nc.vector.memset(wgs[:].rearrange("p s t -> p (s t)").bitcast(I32), 0)
+        nc.vector.memset(wes[:].rearrange("p s t -> p (s t)").bitcast(I32), 0)
+        for plane in second:
+            nc.vector.memset(plane[:].bitcast(I32), 0)
         make_identity(nc, ident[:])
-        nc.gpsimd.memset(wes[:].rearrange("p s t -> p (s t)").bitcast(I32), 0)
         pair_f32 = pairs[:].bitcast(F32)
         pair_u32 = pairs[:].bitcast(U32)
         nc.scalar.copy(pair_f32[:, PAD_BLOCK * C1:(PAD_BLOCK + 1) * C1], zeros[:])
@@ -74,49 +78,42 @@ def tile_moe_hie_none_kernel(
         def load_x(s):
             nc.sync.dma_start(xw[s][:].bitcast(I32), x_words[s].rearrange("p t d -> p (t d)").bitcast(I32))
 
-        def load_wg(f):
-            nc.sync.dma_start(wgw[f][:].bitcast(I32), wg_words[f].rearrange("s p w -> p s w").bitcast(I32))
-
-        def load_we(f):
-            nc.sync.dma_start(
-                wew[f][:].bitcast(I32),
-                we_words[2 * f:2 * f + 2, 0].rearrange("e p n d -> p e (n d)").bitcast(I32),
-            )
-
         nc.sync.dma_start(offs_sb[:], offs)
+        for q in range(4):
+            nc.sync.dma_start(xs[32 * q:32 * q + 8, :].bitcast(I32), x_scales[:, 4 * q:4 * q + 4, :].bitcast(I32))
         load_x(0)
-        load_scales(xs, x_scales)
         load_x(1)
-        load_wg(0)
-        load_scales(wgs0, wg_scales[0])
-        load_wg(1)
-        load_scales(wgs12, wg_scales[1:3].rearrange("f s b i -> (f s) b i"))
+        nc.sync.dma_start(wgw0[:].bitcast(I32), wg_words[0].rearrange("s p w -> p s w").bitcast(I32))
+        load_scales(wgs, wg_scales.rearrange("f s b i -> (f s) b i"))
+        nc.sync.dma_start(wgw12[:].bitcast(I32), wg_words[1:3].rearrange("f s p w -> p (f s) w").bitcast(I32))
         nc.sync.dma_start(offs2_sb[:], offs2)
-        load_wg(2)
-        load_we(0)
         load_scales(wes, we_scales.rearrange("e s b n -> (e s) b n"))
+        nc.sync.dma_start(wew[:].bitcast(I32), we_words[:, 0].rearrange("e p n d -> p e (n d)").bitcast(I32))
         nc.sync.dma_start(dst_sb[:], dst)
         nc.sync.dma_start(gate_sb[:], gate)
-        load_we(1)
-        load_we(2)
+
+        def gather_scales(i):
+            lo, hi = spans[i]
+            nc.vector.tensor_copy(both[i][:], xs[:].indirect(offs_sb[:, lo // 16:hi // 16]))
+            nc.scalar.dma_start(second[i][0:112, :].bitcast(I32), both[i][4:116, :].bitcast(I32))
 
         def group_layer(f):
             cols = offs_sb[:, f * LC:(f + 1) * LC]
             words = kept([P, S, C1], U32, "gw%d" % f)
-            scales = kept([P, S, C1], U8, "gs%d" % f)
             for s in range(S):
                 nc.vector.tensor_copy(words[:, s, :], xw[s][:].indirect(cols))
-                nc.vector.tensor_copy(scales[:, s, :], xs[:, s, :].indirect(cols))
+            planes = (both[min(f, 1)], second[min(f, 1)])
+            start_col = max(f - 1, 0) * C1
             banks = [ps_a.tile([P, H], F32, name="a_bank") for b in range(2)]
             for s in range(S):
-                w_scale = wgs0[:, s, :] if f == 0 else wgs12[:, (f - 1) * S + s, :]
+                w_words = wgw0[:, s, :] if f == 0 else wgw12[:, (f - 1) * S + s, :]
                 for b in range(2):
                     nc.tensor.matmul_mx(
                         out=banks[b][:],
                         lhsT=words[:, s, b * P:(b + 1) * P].bitcast(FP8X4),
-                        lhsT_scale=scales[:, s, b * P:(b + 1) * P],
-                        rhs=wgw[f][:, s, :].bitcast(FP4X4),
-                        rhs_scale=w_scale,
+                        lhsT_scale=planes[s][:, start_col + b * P:start_col + (b + 1) * P],
+                        rhs=w_words.bitcast(FP4X4),
+                        rhs_scale=wgs[:, f * S + s, :],
                         start=(s == 0),
                         stop=(s == S - 1),
                     )
@@ -152,7 +149,7 @@ def tile_moe_hie_none_kernel(
                 for e in range(2):
                     nc.tensor.matmul_mx(
                         out=bank[:, e * C2:(e + 1) * C2],
-                        lhsT=wew[f][:, e, h * P:(h + 1) * P].bitcast(FP8X4),
+                        lhsT=wew[:, 2 * f + e, h * P:(h + 1) * P].bitcast(FP8X4),
                         lhsT_scale=wes[:, 2 * f + e, h * P:(h + 1) * P],
                         rhs=codes[:, e * C2:(e + 1) * C2].bitcast(FP8X4),
                         rhs_scale=scales[:, e * C2:(e + 1) * C2],
@@ -173,7 +170,9 @@ def tile_moe_hie_none_kernel(
                     mult,
                 )
 
+        gather_scales(0)
         group_layer(0)
+        gather_scales(1)
         group_layer(1)
         y0 = expert_layer(0)
         group_layer(2)

@@ -31,9 +31,7 @@ def tile_moe_hie_none_kernel(
 
     with ExitStack() as ctx:
         keep = ctx.enter_context(tc.tile_pool(name="keep", bufs=1))
-        ps_a = ctx.enter_context(tc.psum_pool(name="ps_a", bufs=3))
-        ps_t = ctx.enter_context(tc.psum_pool(name="ps_t", bufs=2))
-        ps_y = ctx.enter_context(tc.psum_pool(name="ps_y", bufs=3))
+        psum = ctx.enter_context(tc.psum_pool(name="psum", bufs=1))
 
         def kept(shape, dtype, name):
             return keep.tile(shape, dtype, name=name, align_bytes=64)
@@ -41,11 +39,12 @@ def tile_moe_hie_none_kernel(
         offs_sb = kept([P, T // 16], U16, "offs_sb")
         offs2_sb = kept([P, T // 16], U16, "offs2_sb")
         dst_sb = kept([P, T // 16], U16, "dst_sb")
-        xw = [kept([P, T], U32, "xw%d" % s) for s in range(S)]
+        xw = kept([P, S, T], U32, "xw")
         xs = kept([P, T], U8, "xs")
         wgw0 = kept([P, S, 2 * H], U8, "wgw0")
         wgw12 = kept([P, 2 * S, 2 * H], U8, "wgw12")
-        wgs = kept([P, G * S, H], U8, "wgs")
+        wgs0 = kept([P, S, H], U8, "wgs0")
+        wgs12 = kept([P, 2 * S, H], U8, "wgs12")
         wew = kept([P, E, N], U32, "wew")
         spans = ((0, C1), (C1, T))
         both = [kept([P, hi - lo], U8, "both%d" % lo) for lo, hi in spans]
@@ -56,13 +55,16 @@ def tile_moe_hie_none_kernel(
         zeros = kept([P, C1], F32, "zeros")
         pairs = kept([P, BLOCKS * 2 * C1], BF16, "pairs")
         res = [kept([P, T], F32, "res%d" % h) for h in range(2)]
+        a_banks = [psum.tile([P, H], F32, name="a_bank%d" % b) for b in range(2)]
+        t_banks = [psum.tile([P, 2 * P], F32, name="t_bank%d" % b) for b in range(2)]
 
         nc.gpsimd.memset(xs[:].bitcast(I32), 0)
-        nc.gpsimd.memset(zeros[:], 0.0)
-        nc.vector.memset(wgs[:].rearrange("p s t -> p (s t)").bitcast(I32), 0)
-        nc.vector.memset(wes[:].rearrange("p s t -> p (s t)").bitcast(I32), 0)
+        nc.vector.memset(wgs0[:].rearrange("p s t -> p (s t)").bitcast(I32), 0)
         for plane in second:
             nc.vector.memset(plane[:].bitcast(I32), 0)
+        nc.vector.memset(wgs12[:].rearrange("p s t -> p (s t)").bitcast(I32), 0)
+        nc.gpsimd.memset(zeros[:], 0.0)
+        nc.gpsimd.memset(wes[:].rearrange("p s t -> p (s t)").bitcast(I32), 0)
         make_identity(nc, ident[:])
         pair_f32 = pairs[:].bitcast(F32)
         pair_u32 = pairs[:].bitcast(U32)
@@ -75,17 +77,14 @@ def tile_moe_hie_none_kernel(
                     rows[:, 4 * q:4 * q + 4, :].rearrange("c r w -> r c w").bitcast(I32),
                 )
 
-        def load_x(s):
-            nc.sync.dma_start(xw[s][:].bitcast(I32), x_words[s].rearrange("p t d -> p (t d)").bitcast(I32))
-
         nc.sync.dma_start(offs_sb[:], offs)
         for q in range(4):
             nc.sync.dma_start(xs[32 * q:32 * q + 8, :].bitcast(I32), x_scales[:, 4 * q:4 * q + 4, :].bitcast(I32))
-        load_x(0)
-        load_x(1)
+        nc.sync.dma_start(xw[:].bitcast(I32), x_words.rearrange("s p t d -> p s (t d)").bitcast(I32))
         nc.sync.dma_start(wgw0[:].bitcast(I32), wg_words[0].rearrange("s p w -> p s w").bitcast(I32))
-        load_scales(wgs, wg_scales.rearrange("f s b i -> (f s) b i"))
+        load_scales(wgs0, wg_scales[0])
         nc.sync.dma_start(wgw12[:].bitcast(I32), wg_words[1:3].rearrange("f s p w -> p (f s) w").bitcast(I32))
+        load_scales(wgs12, wg_scales[1:3].rearrange("f s b i -> (f s) b i"))
         nc.sync.dma_start(offs2_sb[:], offs2)
         load_scales(wes, we_scales.rearrange("e s b n -> (e s) b n"))
         nc.sync.dma_start(wew[:].bitcast(I32), we_words[:, 0].rearrange("e p n d -> p e (n d)").bitcast(I32))
@@ -101,38 +100,38 @@ def tile_moe_hie_none_kernel(
             cols = offs_sb[:, f * LC:(f + 1) * LC]
             words = kept([P, S, C1], U32, "gw%d" % f)
             for s in range(S):
-                nc.vector.tensor_copy(words[:, s, :], xw[s][:].indirect(cols))
+                nc.vector.tensor_copy(words[:, s, :], xw[:, s, :].indirect(cols))
             planes = (both[min(f, 1)], second[min(f, 1)])
             start_col = max(f - 1, 0) * C1
-            banks = [ps_a.tile([P, H], F32, name="a_bank") for b in range(2)]
-            for s in range(S):
-                w_words = wgw0[:, s, :] if f == 0 else wgw12[:, (f - 1) * S + s, :]
-                for b in range(2):
+            rounded = []
+            for b in range(2):
+                for s in range(S):
+                    w_words = wgw0[:, s, :] if f == 0 else wgw12[:, (f - 1) * S + s, :]
+                    w_scales = wgs0[:, s, :] if f == 0 else wgs12[:, (f - 1) * S + s, :]
                     nc.tensor.matmul_mx(
-                        out=banks[b][:],
+                        out=a_banks[b][:],
                         lhsT=words[:, s, b * P:(b + 1) * P].bitcast(FP8X4),
                         lhsT_scale=planes[s][:, start_col + b * P:start_col + (b + 1) * P],
                         rhs=w_words.bitcast(FP4X4),
-                        rhs_scale=wgs[:, f * S + s, :],
+                        rhs_scale=w_scales,
                         start=(s == 0),
                         stop=(s == S - 1),
                     )
-            rounded = []
-            for b in range(2):
                 a_t = kept([P, H], BF16, "aT%d_%d" % (f, b))
                 nc.scalar.copy(
                     a_t[:].rearrange("m (u p e) -> m u p e", u=2, e=2),
-                    banks[b][:].rearrange("m (p u e) -> m u p e", u=2, e=2),
+                    a_banks[b][:].rearrange("m (p u e) -> m u p e", u=2, e=2),
                 )
                 rounded.append(a_t)
             home = pair_f32[:, FIRST_BLOCK[f] * C1:(FIRST_BLOCK[f] + 2) * C1].rearrange("p (u j) -> p u j", u=2)
             for b in range(2):
-                turned = ps_t.tile([P, 2, P], F32, name="turned")
                 for u in range(2):
-                    nc.tensor.transpose(turned[:, u, :], rounded[b][:].bitcast(F32)[:, u * P:(u + 1) * P], ident[:])
-                nc.scalar.copy(home[:, :, b * P:(b + 1) * P], turned[:])
+                    nc.tensor.transpose(
+                        t_banks[b][:, u * P:(u + 1) * P], rounded[b][:].bitcast(F32)[:, u * P:(u + 1) * P], ident[:]
+                    )
+                nc.scalar.copy(home[:, :, b * P:(b + 1) * P], t_banks[b][:].rearrange("p (u j) -> p u j", u=2))
 
-        def expert_layer(f):
+        def quantise(f):
             cols = offs2_sb[:, f * LC:(f + 1) * LC]
             picked = kept([P, 4 * C1], BF16, "picked%d" % f)
             picked_u32 = picked[:].bitcast(U32).rearrange("p (m u) -> p m u", u=2)
@@ -143,9 +142,12 @@ def tile_moe_hie_none_kernel(
             codes = kept([P, C1], U32, "codes%d" % f)
             scales = kept([P, C1], U8, "ascale%d" % f)
             nc.vector.quantize_mx(out=codes[:].bitcast(FP8X4), scales=scales[:], in_=picked[:])
+            return codes, scales
+
+        def expert_layer(f, codes, scales):
             ys = []
             for h in range(2):
-                bank = ps_y.tile([P, C1], F32, name="y_bank")
+                bank = t_banks[1 - h]
                 for e in range(2):
                     nc.tensor.matmul_mx(
                         out=bank[:, e * C2:(e + 1) * C2],
@@ -171,15 +173,14 @@ def tile_moe_hie_none_kernel(
                 )
 
         gather_scales(0)
-        group_layer(0)
         gather_scales(1)
-        group_layer(1)
-        y0 = expert_layer(0)
-        group_layer(2)
-        y1 = expert_layer(1)
-        send_home(0, y0)
-        y2 = expert_layer(2)
-        send_home(1, y1)
-        send_home(2, y2)
+        quantised = []
+        for f in range(G):
+            group_layer(f)
+        for f in range(G):
+            quantised.append(quantise(f))
+        results = [expert_layer(f, *quantised[f]) for f in range(G)]
+        for f in range(G):
+            send_home(f, results[f])
         for h in range(2):
             nc.sync.dma_start(out[h * P:(h + 1) * P, :], res[h][:])

@@ -55,7 +55,7 @@ def tile_moe_hie_none_kernel(
         zeros = kept([P, C1], F32, "zeros")
         pairs = kept([P, BLOCKS * 2 * C1], BF16, "pairs")
         res = [kept([P, T], F32, "res%d" % h) for h in range(2)]
-        a_banks = [psum.tile([P, H], F32, name="a_bank%d" % b) for b in range(2)]
+        a_banks = [psum.tile([P, H], F32, name="a_bank%d" % b) for b in range(4)]
         t_banks = [psum.tile([P, 2 * P], F32, name="t_bank%d" % b) for b in range(2)]
 
         nc.gpsimd.memset(xs[:].bitcast(I32), 0)
@@ -109,7 +109,7 @@ def tile_moe_hie_none_kernel(
                     w_words = wgw0[:, s, :] if f == 0 else wgw12[:, (f - 1) * S + s, :]
                     w_scales = wgs0[:, s, :] if f == 0 else wgs12[:, (f - 1) * S + s, :]
                     nc.tensor.matmul_mx(
-                        out=a_banks[b][:],
+                        out=a_banks[2 * (f % 2) + b][:],
                         lhsT=words[:, s, b * P:(b + 1) * P].bitcast(FP8X4),
                         lhsT_scale=planes[s][:, start_col + b * P:start_col + (b + 1) * P],
                         rhs=w_words.bitcast(FP4X4),
@@ -120,9 +120,12 @@ def tile_moe_hie_none_kernel(
                 a_t = kept([P, H], BF16, "aT%d_%d" % (f, b))
                 nc.scalar.copy(
                     a_t[:].rearrange("m (u p e) -> m u p e", u=2, e=2),
-                    a_banks[b][:].rearrange("m (p u e) -> m u p e", u=2, e=2),
+                    a_banks[2 * (f % 2) + b][:].rearrange("m (p u e) -> m u p e", u=2, e=2),
                 )
                 rounded.append(a_t)
+            return rounded
+
+        def turn(f, rounded):
             home = pair_f32[:, FIRST_BLOCK[f] * C1:(FIRST_BLOCK[f] + 2) * C1].rearrange("p (u j) -> p u j", u=2)
             for b in range(2):
                 for u in range(2):
@@ -174,13 +177,18 @@ def tile_moe_hie_none_kernel(
 
         gather_scales(0)
         gather_scales(1)
-        quantised = []
-        for f in range(G):
-            group_layer(f)
-        for f in range(G):
-            quantised.append(quantise(f))
-        results = [expert_layer(f, *quantised[f]) for f in range(G)]
-        for f in range(G):
-            send_home(f, results[f])
+        turn(0, group_layer(0))
+        turn(1, group_layer(1))
+        last_rounded = group_layer(2)
+        quantised0 = quantise(0)
+        quantised1 = quantise(1)
+        y0 = expert_layer(0, *quantised0)
+        turn(2, last_rounded)
+        send_home(0, y0)
+        quantised2 = quantise(2)
+        y1 = expert_layer(1, *quantised1)
+        y2 = expert_layer(2, *quantised2)
+        send_home(1, y1)
+        send_home(2, y2)
         for h in range(2):
             nc.sync.dma_start(out[h * P:(h + 1) * P, :], res[h][:])

@@ -18,7 +18,7 @@ FP4X4 = mybir.dt.float4_e2m1fn_x4
 P = 128
 S = K // 512
 LC = C1 // 16
-FIRST_BLOCK = (0, 3, 5)
+HOME_BLOCK = ((1, 0), (3, 4), (5, 6))
 PAD_BLOCK = 2
 BLOCKS = 7
 
@@ -43,8 +43,7 @@ def tile_moe_hie_none_kernel(
         xs = kept([P, T], U8, "xs")
         wgw0 = kept([P, S, 2 * H], U8, "wgw0")
         wgw12 = kept([P, 2 * S, 2 * H], U8, "wgw12")
-        wgs0 = kept([P, S, H], U8, "wgs0")
-        wgs12 = kept([P, 2 * S, H], U8, "wgs12")
+        wgs = kept([P, G * S, H], U8, "wgs")
         wew = kept([P, E, N], U32, "wew")
         spans = ((0, C1), (C1, T))
         both = [kept([P, hi - lo], U8, "both%d" % lo) for lo, hi in spans]
@@ -54,15 +53,14 @@ def tile_moe_hie_none_kernel(
         ident = kept([P, P], F32, "ident")
         zeros = kept([P, C1], F32, "zeros")
         pairs = kept([P, BLOCKS * 2 * C1], BF16, "pairs")
-        res = [kept([P, T], F32, "res%d" % h) for h in range(2)]
-        a_banks = [psum.tile([P, H], F32, name="a_bank%d" % b) for b in range(4)]
-        t_banks = [psum.tile([P, 2 * P], F32, name="t_bank%d" % b) for b in range(2)]
+        banks = [psum.tile([P, H], F32, name="bank%d" % b) for b in range(8)]
+        a_banks = (banks[0:2], banks[2:4], banks[4:6])
+        t_banks = banks[6:8]
 
         nc.gpsimd.memset(xs[:].bitcast(I32), 0)
-        nc.vector.memset(wgs0[:].rearrange("p s t -> p (s t)").bitcast(I32), 0)
+        nc.vector.memset(wgs[:].rearrange("p s t -> p (s t)").bitcast(I32), 0)
         for plane in second:
             nc.vector.memset(plane[:].bitcast(I32), 0)
-        nc.vector.memset(wgs12[:].rearrange("p s t -> p (s t)").bitcast(I32), 0)
         nc.gpsimd.memset(zeros[:], 0.0)
         nc.gpsimd.memset(wes[:].rearrange("p s t -> p (s t)").bitcast(I32), 0)
         make_identity(nc, ident[:])
@@ -82,9 +80,8 @@ def tile_moe_hie_none_kernel(
             nc.sync.dma_start(xs[32 * q:32 * q + 8, :].bitcast(I32), x_scales[:, 4 * q:4 * q + 4, :].bitcast(I32))
         nc.sync.dma_start(xw[:].bitcast(I32), x_words.rearrange("s p t d -> p s (t d)").bitcast(I32))
         nc.sync.dma_start(wgw0[:].bitcast(I32), wg_words[0].rearrange("s p w -> p s w").bitcast(I32))
-        load_scales(wgs0, wg_scales[0])
+        load_scales(wgs, wg_scales.rearrange("f s b i -> (f s) b i"))
         nc.sync.dma_start(wgw12[:].bitcast(I32), wg_words[1:3].rearrange("f s p w -> p (f s) w").bitcast(I32))
-        load_scales(wgs12, wg_scales[1:3].rearrange("f s b i -> (f s) b i"))
         nc.sync.dma_start(offs2_sb[:], offs2)
         load_scales(wes, we_scales.rearrange("e s b n -> (e s) b n"))
         nc.sync.dma_start(wew[:].bitcast(I32), we_words[:, 0].rearrange("e p n d -> p e (n d)").bitcast(I32))
@@ -103,46 +100,49 @@ def tile_moe_hie_none_kernel(
                 nc.vector.tensor_copy(words[:, s, :], xw[:, s, :].indirect(cols))
             planes = (both[min(f, 1)], second[min(f, 1)])
             start_col = max(f - 1, 0) * C1
-            rounded = []
-            for b in range(2):
-                for s in range(S):
-                    w_words = wgw0[:, s, :] if f == 0 else wgw12[:, (f - 1) * S + s, :]
-                    w_scales = wgs0[:, s, :] if f == 0 else wgs12[:, (f - 1) * S + s, :]
+            for s in range(S):
+                w_words = wgw0[:, s, :] if f == 0 else wgw12[:, (f - 1) * S + s, :]
+                for b in range(2):
                     nc.tensor.matmul_mx(
-                        out=a_banks[2 * (f % 2) + b][:],
+                        out=a_banks[f][b][:],
                         lhsT=words[:, s, b * P:(b + 1) * P].bitcast(FP8X4),
                         lhsT_scale=planes[s][:, start_col + b * P:start_col + (b + 1) * P],
                         rhs=w_words.bitcast(FP4X4),
-                        rhs_scale=w_scales,
+                        rhs_scale=wgs[:, f * S + s, :],
                         start=(s == 0),
                         stop=(s == S - 1),
                     )
-                a_t = kept([P, H], BF16, "aT%d_%d" % (f, b))
-                nc.scalar.copy(
-                    a_t[:].rearrange("m (u p e) -> m u p e", u=2, e=2),
-                    a_banks[2 * (f % 2) + b][:].rearrange("m (p u e) -> m u p e", u=2, e=2),
-                )
-                rounded.append(a_t)
+
+        def round_out(f, tag):
+            rounded = keep.tile([P, 2 * H], BF16, name="aT%d" % f, tag=tag, align_bytes=64)
+            sorted_out = rounded[:].rearrange("m (b u p e) -> m b u p e", b=2, u=2, e=2)
+            sorted_in = [bank[:].rearrange("m (p u e) -> m u p e", u=2, e=2) for bank in a_banks[f]]
+            nc.scalar.copy(sorted_out[:, 0], sorted_in[0])
+            for u in range(2):
+                nc.scalar.copy(sorted_out[:, 1, u], sorted_in[1][:, u])
             return rounded
 
         def turn(f, rounded):
-            home = pair_f32[:, FIRST_BLOCK[f] * C1:(FIRST_BLOCK[f] + 2) * C1].rearrange("p (u j) -> p u j", u=2)
             for b in range(2):
                 for u in range(2):
                     nc.tensor.transpose(
-                        t_banks[b][:, u * P:(u + 1) * P], rounded[b][:].bitcast(F32)[:, u * P:(u + 1) * P], ident[:]
+                        t_banks[u][:, b * P:(b + 1) * P],
+                        rounded[:].bitcast(F32)[:, (2 * b + u) * P:(2 * b + u + 1) * P],
+                        ident[:],
                     )
-                nc.scalar.copy(home[:, :, b * P:(b + 1) * P], t_banks[b][:].rearrange("p (u j) -> p u j", u=2))
+            for u in range(2):
+                first = HOME_BLOCK[f][u] * C1
+                nc.scalar.copy(pair_f32[:, first:first + C1], t_banks[u][:, 0:C1])
 
         def quantise(f):
             cols = offs2_sb[:, f * LC:(f + 1) * LC]
-            picked = kept([P, 4 * C1], BF16, "picked%d" % f)
+            picked = keep.tile([P, 4 * C1], BF16, name="picked%d" % f, tag="picked%d" % f, align_bytes=64)
             picked_u32 = picked[:].bitcast(U32).rearrange("p (m u) -> p m u", u=2)
             for u in range(2):
-                first = (FIRST_BLOCK[f] + u - f) * C1
+                first = (HOME_BLOCK[f][u] - f) * C1
                 width = max(2, f + 1) * C1
                 nc.vector.tensor_copy(picked_u32[:, :, u], pair_u32[:, first:first + width].indirect(cols))
-            codes = kept([P, C1], U32, "codes%d" % f)
+            codes = keep.tile([P, C1], U32, name="codes%d" % f, tag="codes%d" % f, align_bytes=64)
             scales = kept([P, C1], U8, "ascale%d" % f)
             nc.vector.quantize_mx(out=codes[:].bitcast(FP8X4), scales=scales[:], in_=picked[:])
             return codes, scales
@@ -150,7 +150,7 @@ def tile_moe_hie_none_kernel(
         def expert_layer(f, codes, scales):
             ys = []
             for h in range(2):
-                bank = t_banks[1 - h]
+                bank = a_banks[f][h]
                 for e in range(2):
                     nc.tensor.matmul_mx(
                         out=bank[:, e * C2:(e + 1) * C2],
@@ -161,34 +161,39 @@ def tile_moe_hie_none_kernel(
                         start=True,
                         stop=True,
                     )
-                y = kept([P, C1], F32, "y%d_%d" % (f, h))
-                nc.scalar.copy(y[:], bank[:])
+                tag = "picked2" if (f, h) == (0, 0) else "y%d_%d" % (f, h)
+                y = keep.tile([P, C1], F32, name="y%d_%d" % (f, h), tag=tag, align_bytes=64)
+                nc.scalar.copy(y[:], bank[:, 0:C1])
                 ys.append(y)
             return ys
 
-        def send_home(f, ys):
-            for h in range(2):
-                nc.vector.tensor_tensor(
-                    res[h][:].indirect(dst_sb[:, f * LC:(f + 1) * LC]),
-                    ys[h][:],
-                    gate_sb[:, f * C1:(f + 1) * C1],
-                    mult,
-                )
+        def send_home(f, h, y, home):
+            nc.vector.tensor_tensor(
+                home[:].indirect(dst_sb[:, f * LC:(f + 1) * LC]),
+                y[h][:],
+                gate_sb[:, f * C1:(f + 1) * C1],
+                mult,
+            )
 
         gather_scales(0)
         gather_scales(1)
-        turn(0, group_layer(0))
-        turn(1, group_layer(1))
-        last_rounded = group_layer(2)
+        for f in range(2):
+            group_layer(f)
+            turn(f, round_out(f, "aT%d" % f))
+        group_layer(2)
         quantised0 = quantise(0)
         quantised1 = quantise(1)
         y0 = expert_layer(0, *quantised0)
-        turn(2, last_rounded)
-        send_home(0, y0)
-        quantised2 = quantise(2)
+        turn(2, round_out(2, "codes0"))
         y1 = expert_layer(1, *quantised1)
-        y2 = expert_layer(2, *quantised2)
-        send_home(1, y1)
-        send_home(2, y2)
-        for h in range(2):
-            nc.sync.dma_start(out[h * P:(h + 1) * P, :], res[h][:])
+        upper = kept([P, T], F32, "upper")
+        send_home(0, 0, y0, upper)
+        send_home(1, 0, y1, upper)
+        y2 = expert_layer(2, *quantise(2))
+        lower = keep.tile([P, T], F32, name="lower", tag="picked2", align_bytes=64)
+        send_home(0, 1, y0, lower)
+        send_home(1, 1, y1, lower)
+        send_home(2, 0, y2, upper)
+        send_home(2, 1, y2, lower)
+        nc.sync.dma_start(out[0:P, :], upper[:])
+        nc.sync.dma_start(out[P:2 * P, :], lower[:])

@@ -43,7 +43,8 @@ def tile_moe_hie_none_kernel(
         xs = kept([P, T], U8, "xs")
         wgw0 = kept([P, S, 2 * H], U8, "wgw0")
         wgw12 = kept([P, 2 * S, 2 * H], U8, "wgw12")
-        wgs = kept([P, G * S, H], U8, "wgs")
+        wgs0 = kept([P, S, H], U8, "wgs0")
+        wgs12 = kept([P, 2 * S, H], U8, "wgs12")
         wew = kept([P, E, N], U32, "wew")
         spans = ((0, C1), (C1, T))
         both = [kept([P, hi - lo], U8, "both%d" % lo) for lo, hi in spans]
@@ -58,9 +59,10 @@ def tile_moe_hie_none_kernel(
         t_banks = banks[6:8]
 
         nc.gpsimd.memset(xs[:].bitcast(I32), 0)
-        nc.vector.memset(wgs[:].rearrange("p s t -> p (s t)").bitcast(I32), 0)
+        nc.vector.memset(wgs0[:].rearrange("p s t -> p (s t)").bitcast(I32), 0)
         for plane in second:
             nc.vector.memset(plane[:].bitcast(I32), 0)
+        nc.vector.memset(wgs12[:].rearrange("p s t -> p (s t)").bitcast(I32), 0)
         nc.gpsimd.memset(zeros[:], 0.0)
         nc.gpsimd.memset(wes[:].rearrange("p s t -> p (s t)").bitcast(I32), 0)
         make_identity(nc, ident[:])
@@ -80,8 +82,9 @@ def tile_moe_hie_none_kernel(
             nc.sync.dma_start(xs[32 * q:32 * q + 8, :].bitcast(I32), x_scales[:, 4 * q:4 * q + 4, :].bitcast(I32))
         nc.sync.dma_start(xw[:].bitcast(I32), x_words.rearrange("s p t d -> p s (t d)").bitcast(I32))
         nc.sync.dma_start(wgw0[:].bitcast(I32), wg_words[0].rearrange("s p w -> p s w").bitcast(I32))
-        load_scales(wgs, wg_scales.rearrange("f s b i -> (f s) b i"))
+        load_scales(wgs0, wg_scales[0])
         nc.sync.dma_start(wgw12[:].bitcast(I32), wg_words[1:3].rearrange("f s p w -> p (f s) w").bitcast(I32))
+        load_scales(wgs12, wg_scales[1:3].rearrange("f s b i -> (f s) b i"))
         nc.sync.dma_start(offs2_sb[:], offs2)
         load_scales(wes, we_scales.rearrange("e s b n -> (e s) b n"))
         nc.sync.dma_start(wew[:].bitcast(I32), we_words[:, 0].rearrange("e p n d -> p e (n d)").bitcast(I32))
@@ -102,13 +105,14 @@ def tile_moe_hie_none_kernel(
             start_col = max(f - 1, 0) * C1
             for s in range(S):
                 w_words = wgw0[:, s, :] if f == 0 else wgw12[:, (f - 1) * S + s, :]
+                w_scales = wgs0[:, s, :] if f == 0 else wgs12[:, (f - 1) * S + s, :]
                 for b in range(2):
                     nc.tensor.matmul_mx(
                         out=a_banks[f][b][:],
                         lhsT=words[:, s, b * P:(b + 1) * P].bitcast(FP8X4),
                         lhsT_scale=planes[s][:, start_col + b * P:start_col + (b + 1) * P],
                         rhs=w_words.bitcast(FP4X4),
-                        rhs_scale=wgs[:, f * S + s, :],
+                        rhs_scale=w_scales,
                         start=(s == 0),
                         stop=(s == S - 1),
                     )

@@ -43,8 +43,8 @@ def tile_moe_hie_none_kernel(
         xs = kept([P, T], U8, "xs")
         wgw0 = kept([P, S, 2 * H], U8, "wgw0")
         wgw12 = kept([P, 2 * S, 2 * H], U8, "wgw12")
-        wgs0 = kept([P, S, H], U8, "wgs0")
-        wgs12 = kept([P, 2 * S, H], U8, "wgs12")
+        wgs01 = kept([P, 2 * S, H], U8, "wgs01")
+        wgs2 = kept([P, S, H], U8, "wgs2")
         wew = kept([P, E, N], U32, "wew")
         spans = ((0, C1), (C1, T))
         both = [kept([P, hi - lo], U8, "both%d" % lo) for lo, hi in spans]
@@ -59,10 +59,10 @@ def tile_moe_hie_none_kernel(
         t_banks = banks[6:8]
 
         nc.gpsimd.memset(xs[:].bitcast(I32), 0)
-        nc.vector.memset(wgs0[:].rearrange("p s t -> p (s t)").bitcast(I32), 0)
+        nc.vector.memset(wgs01[:].rearrange("p s t -> p (s t)").bitcast(I32), 0)
         for plane in second:
             nc.vector.memset(plane[:].bitcast(I32), 0)
-        nc.vector.memset(wgs12[:].rearrange("p s t -> p (s t)").bitcast(I32), 0)
+        nc.vector.memset(wgs2[:].rearrange("p s t -> p (s t)").bitcast(I32), 0)
         nc.gpsimd.memset(zeros[:], 0.0)
         nc.gpsimd.memset(wes[:].rearrange("p s t -> p (s t)").bitcast(I32), 0)
         make_identity(nc, ident[:])
@@ -82,12 +82,12 @@ def tile_moe_hie_none_kernel(
             nc.sync.dma_start(xs[32 * q:32 * q + 8, :].bitcast(I32), x_scales[:, 4 * q:4 * q + 4, :].bitcast(I32))
         nc.sync.dma_start(xw[:].bitcast(I32), x_words.rearrange("s p t d -> p s (t d)").bitcast(I32))
         nc.sync.dma_start(wgw0[:].bitcast(I32), wg_words[0].rearrange("s p w -> p s w").bitcast(I32))
-        load_scales(wgs0, wg_scales[0])
+        load_scales(wgs01, wg_scales[0:2].rearrange("f s b i -> (f s) b i"))
         nc.sync.dma_start(wgw12[:].bitcast(I32), wg_words[1:3].rearrange("f s p w -> p (f s) w").bitcast(I32))
-        load_scales(wgs12, wg_scales[1:3].rearrange("f s b i -> (f s) b i"))
         nc.sync.dma_start(offs2_sb[:], offs2)
-        load_scales(wes, we_scales.rearrange("e s b n -> (e s) b n"))
+        load_scales(wgs2, wg_scales[2])
         nc.sync.dma_start(wew[:].bitcast(I32), we_words[:, 0].rearrange("e p n d -> p e (n d)").bitcast(I32))
+        load_scales(wes, we_scales.rearrange("e s b n -> (e s) b n"))
         nc.sync.dma_start(dst_sb[:], dst)
         nc.sync.dma_start(gate_sb[:], gate)
 
@@ -105,7 +105,7 @@ def tile_moe_hie_none_kernel(
             start_col = max(f - 1, 0) * C1
             for s in range(S):
                 w_words = wgw0[:, s, :] if f == 0 else wgw12[:, (f - 1) * S + s, :]
-                w_scales = wgs0[:, s, :] if f == 0 else wgs12[:, (f - 1) * S + s, :]
+                w_scales = wgs01[:, f * S + s, :] if f < 2 else wgs2[:, s, :]
                 for b in range(2):
                     nc.tensor.matmul_mx(
                         out=a_banks[f][b][:],
@@ -136,7 +136,10 @@ def tile_moe_hie_none_kernel(
                     )
             for u in range(2):
                 first = HOME_BLOCK[f][u] * C1
-                nc.scalar.copy(pair_f32[:, first:first + C1], t_banks[u][:, 0:C1])
+                if f == 0:
+                    nc.vector.tensor_copy(pair_f32[:, first:first + C1], t_banks[u][:, 0:C1])
+                else:
+                    nc.scalar.copy(pair_f32[:, first:first + C1], t_banks[u][:, 0:C1])
 
         def quantise(f):
             cols = offs2_sb[:, f * LC:(f + 1) * LC]

@@ -57,6 +57,7 @@ def tile_moe_hie_none_kernel(
         banks = [psum.tile([P, H], F32, name="bank%d" % b) for b in range(8)]
         a_banks = (banks[0:2], banks[2:4], banks[4:6])
         t_banks = banks[6:8]
+        y_banks = (a_banks[0], (t_banks[1], t_banks[0]), a_banks[1])
 
         nc.gpsimd.memset(xs[:].bitcast(I32), 0)
         nc.vector.memset(wgs01[:].rearrange("p s t -> p (s t)").bitcast(I32), 0)
@@ -143,7 +144,7 @@ def tile_moe_hie_none_kernel(
 
         def quantise(f):
             cols = offs2_sb[:, f * LC:(f + 1) * LC]
-            picked = keep.tile([P, 4 * C1], BF16, name="picked%d" % f, tag="picked%d" % f, align_bytes=64)
+            picked = kept([P, 4 * C1], BF16, "picked%d" % f)
             picked_u32 = picked[:].bitcast(U32).rearrange("p (m u) -> p m u", u=2)
             for u in range(2):
                 first = (HOME_BLOCK[f][u] - f) * C1
@@ -157,7 +158,7 @@ def tile_moe_hie_none_kernel(
         def expert_layer(f, codes, scales):
             ys = []
             for h in range(2):
-                bank = a_banks[f][h]
+                bank = y_banks[f][h]
                 for e in range(2):
                     nc.tensor.matmul_mx(
                         out=bank[:, e * C2:(e + 1) * C2],
@@ -168,8 +169,7 @@ def tile_moe_hie_none_kernel(
                         start=True,
                         stop=True,
                     )
-                tag = "picked2" if (f, h) == (0, 0) else "y%d_%d" % (f, h)
-                y = keep.tile([P, C1], F32, name="y%d_%d" % (f, h), tag=tag, align_bytes=64)
+                y = kept([P, C1], F32, "y%d_%d" % (f, h))
                 nc.scalar.copy(y[:], bank[:, 0:C1])
                 ys.append(y)
             return ys
@@ -192,15 +192,15 @@ def tile_moe_hie_none_kernel(
         quantised1 = quantise(1)
         y0 = expert_layer(0, *quantised0)
         turn(2, round_out(2, "codes0"))
+        res = [kept([P, T], F32, "res%d" % h) for h in range(2)]
+        for h in range(2):
+            send_home(0, h, y0, res[h])
+        quantised2 = quantise(2)
         y1 = expert_layer(1, *quantised1)
-        upper = kept([P, T], F32, "upper")
-        send_home(0, 0, y0, upper)
-        send_home(1, 0, y1, upper)
-        y2 = expert_layer(2, *quantise(2))
-        lower = keep.tile([P, T], F32, name="lower", tag="picked2", align_bytes=64)
-        send_home(0, 1, y0, lower)
-        send_home(1, 1, y1, lower)
-        send_home(2, 0, y2, upper)
-        send_home(2, 1, y2, lower)
-        nc.sync.dma_start(out[0:P, :], upper[:])
-        nc.sync.dma_start(out[P:2 * P, :], lower[:])
+        y2 = expert_layer(2, *quantised2)
+        for h in range(2):
+            send_home(1, h, y1, res[h])
+        for h in range(2):
+            send_home(2, h, y2, res[h])
+        for h in range(2):
+            nc.sync.dma_start(out[h * P:(h + 1) * P, :], res[h][:])

@@ -53,11 +53,11 @@ def tile_moe_hie_none_kernel(
         gate_sb = kept([P, T], F32, "gate_sb")
         ident = kept([P, P], F32, "ident")
         zeros = kept([P, C1], F32, "zeros")
-        pairs = kept([P, BLOCKS * 2 * C1], BF16, "pairs")
+        pairs = keep.tile([P, BLOCKS * 2 * C1], BF16, name="pairs", tag="pairs", align_bytes=64)
         banks = [psum.tile([P, H], F32, name="bank%d" % b) for b in range(8)]
         a_banks = (banks[0:2], banks[2:4], banks[4:6])
         t_banks = banks[6:8]
-        y_banks = (a_banks[0], (t_banks[1], t_banks[0]), a_banks[1])
+        y_banks = (t_banks, a_banks[0], a_banks[1])
 
         nc.gpsimd.memset(xs[:].bitcast(I32), 0)
         nc.vector.memset(wgs01[:].rearrange("p s t -> p (s t)").bitcast(I32), 0)
@@ -137,31 +137,40 @@ def tile_moe_hie_none_kernel(
                     )
             for u in range(2):
                 first = HOME_BLOCK[f][u] * C1
-                if f == 0:
-                    nc.vector.tensor_copy(pair_f32[:, first:first + C1], t_banks[u][:, 0:C1])
-                else:
+                if f < 2:
                     nc.scalar.copy(pair_f32[:, first:first + C1], t_banks[u][:, 0:C1])
+                else:
+                    nc.scalar.copy(
+                        pairs[:, 2 * first:2 * (first + C1)].rearrange("p (e j) -> p e j", e=2),
+                        t_banks[u][:, 0:C1].bitcast(BF16).rearrange("p (j e) -> p e j", e=2),
+                    )
 
         def quantise(f):
             cols = offs2_sb[:, f * LC:(f + 1) * LC]
             picked = kept([P, 4 * C1], BF16, "picked%d" % f)
             picked_u32 = picked[:].bitcast(U32).rearrange("p (m u) -> p m u", u=2)
-            for u in range(2):
-                first = (HOME_BLOCK[f][u] - f) * C1
-                width = max(2, f + 1) * C1
-                nc.vector.tensor_copy(picked_u32[:, :, u], pair_u32[:, first:first + width].indirect(cols))
+            if f < 2:
+                for u in range(2):
+                    first = (HOME_BLOCK[f][u] - f) * C1
+                    nc.vector.tensor_copy(picked_u32[:, :, u], pair_u32[:, first:first + 2 * C1].indirect(cols))
+            else:
+                for t in range(4):
+                    first = (2 * HOME_BLOCK[f][0] + t - f) * C1
+                    nc.scalar.activation(
+                        picked[:].rearrange("p (m t) -> p m t", t=4)[:, :, t],
+                        pairs[:, first:first + T].indirect(cols),
+                        mybir.ActivationFunctionType.Copy,
+                    )
             codes = keep.tile([P, C1], U32, name="codes%d" % f, tag="codes%d" % f, align_bytes=64)
             scales = kept([P, C1], U8, "ascale%d" % f)
             nc.vector.quantize_mx(out=codes[:].bitcast(FP8X4), scales=scales[:], in_=picked[:])
             return codes, scales
 
         def expert_layer(f, codes, scales):
-            ys = []
             for h in range(2):
-                bank = y_banks[f][h]
                 for e in range(2):
                     nc.tensor.matmul_mx(
-                        out=bank[:, e * C2:(e + 1) * C2],
+                        out=y_banks[f][h][:, e * C2:(e + 1) * C2],
                         lhsT=wew[:, 2 * f + e, h * P:(h + 1) * P].bitcast(FP8X4),
                         lhsT_scale=wes[:, 2 * f + e, h * P:(h + 1) * P],
                         rhs=codes[:, e * C2:(e + 1) * C2].bitcast(FP8X4),
@@ -169,15 +178,16 @@ def tile_moe_hie_none_kernel(
                         start=True,
                         stop=True,
                     )
-                y = kept([P, C1], F32, "y%d_%d" % (f, h))
-                nc.scalar.copy(y[:], bank[:, 0:C1])
-                ys.append(y)
-            return ys
 
-        def send_home(f, h, y, home):
+        def results(f, h, tag):
+            y = keep.tile([P, C1], F32, name="y%d_%d" % (f, h), tag=tag, align_bytes=64)
+            nc.scalar.copy(y[:], y_banks[f][h][:, 0:C1])
+            return y
+
+        def send_home(f, y, home):
             nc.vector.tensor_tensor(
                 home[:].indirect(dst_sb[:, f * LC:(f + 1) * LC]),
-                y[h][:],
+                y[:],
                 gate_sb[:, f * C1:(f + 1) * C1],
                 mult,
             )
@@ -188,19 +198,21 @@ def tile_moe_hie_none_kernel(
             group_layer(f)
             turn(f, round_out(f, "aT%d" % f))
         group_layer(2)
+        last_rounded = round_out(2, "aT2")
         quantised0 = quantise(0)
         quantised1 = quantise(1)
-        y0 = expert_layer(0, *quantised0)
-        turn(2, round_out(2, "codes0"))
         res = [kept([P, T], F32, "res%d" % h) for h in range(2)]
+        expert_layer(0, *quantised0)
+        y0 = [results(0, h, "y0_%d" % h) for h in range(2)]
+        expert_layer(1, *quantised1)
+        upper1 = results(1, 0, "y1_0")
+        turn(2, last_rounded)
         for h in range(2):
-            send_home(0, h, y0, res[h])
-        quantised2 = quantise(2)
-        y1 = expert_layer(1, *quantised1)
-        y2 = expert_layer(2, *quantised2)
+            send_home(0, y0[h], res[h])
+        send_home(1, upper1, res[0])
+        expert_layer(2, *quantise(2))
+        send_home(1, results(1, 1, "pairs"), res[1])
         for h in range(2):
-            send_home(1, h, y1, res[h])
-        for h in range(2):
-            send_home(2, h, y2, res[h])
+            send_home(2, results(2, h, "y2_%d" % h), res[h])
         for h in range(2):
             nc.sync.dma_start(out[h * P:(h + 1) * P, :], res[h][:])

@@ -43,8 +43,8 @@ def tile_moe_hie_none_kernel(
         xs = kept([P, T], U8, "xs")
         wgw0 = kept([P, S, 2 * H], U8, "wgw0")
         wgw12 = kept([P, 2 * S, 2 * H], U8, "wgw12")
-        wgs01 = kept([P, 2 * S, H], U8, "wgs01")
-        wgs2 = kept([P, S, H], U8, "wgs2")
+        wgs0 = kept([P, S, H], U8, "wgs0")
+        wgs12 = kept([P, 2 * S, H], U8, "wgs12")
         wew = kept([P, E, N], U32, "wew")
         spans = ((0, C1), (C1, T))
         both = [kept([P, hi - lo], U8, "both%d" % lo) for lo, hi in spans]
@@ -57,13 +57,13 @@ def tile_moe_hie_none_kernel(
         banks = [psum.tile([P, H], F32, name="bank%d" % b) for b in range(8)]
         a_banks = (banks[0:2], banks[2:4], banks[4:6])
         t_banks = banks[6:8]
-        y_banks = (t_banks, a_banks[0], a_banks[1])
+        y_banks = (t_banks, t_banks, a_banks[0])
 
         nc.gpsimd.memset(xs[:].bitcast(I32), 0)
-        nc.vector.memset(wgs01[:].rearrange("p s t -> p (s t)").bitcast(I32), 0)
+        nc.vector.memset(wgs0[:].rearrange("p s t -> p (s t)").bitcast(I32), 0)
         for plane in second:
             nc.vector.memset(plane[:].bitcast(I32), 0)
-        nc.vector.memset(wgs2[:].rearrange("p s t -> p (s t)").bitcast(I32), 0)
+        nc.vector.memset(wgs12[:].rearrange("p s t -> p (s t)").bitcast(I32), 0)
         nc.gpsimd.memset(zeros[:], 0.0)
         nc.gpsimd.memset(wes[:].rearrange("p s t -> p (s t)").bitcast(I32), 0)
         make_identity(nc, ident[:])
@@ -83,10 +83,10 @@ def tile_moe_hie_none_kernel(
             nc.sync.dma_start(xs[32 * q:32 * q + 8, :].bitcast(I32), x_scales[:, 4 * q:4 * q + 4, :].bitcast(I32))
         nc.sync.dma_start(xw[:].bitcast(I32), x_words.rearrange("s p t d -> p s (t d)").bitcast(I32))
         nc.sync.dma_start(wgw0[:].bitcast(I32), wg_words[0].rearrange("s p w -> p s w").bitcast(I32))
-        load_scales(wgs01, wg_scales[0:2].rearrange("f s b i -> (f s) b i"))
+        load_scales(wgs0, wg_scales[0])
         nc.sync.dma_start(wgw12[:].bitcast(I32), wg_words[1:3].rearrange("f s p w -> p (f s) w").bitcast(I32))
+        load_scales(wgs12, wg_scales[1:3].rearrange("f s b i -> (f s) b i"))
         nc.sync.dma_start(offs2_sb[:], offs2)
-        load_scales(wgs2, wg_scales[2])
         nc.sync.dma_start(wew[:].bitcast(I32), we_words[:, 0].rearrange("e p n d -> p e (n d)").bitcast(I32))
         load_scales(wes, we_scales.rearrange("e s b n -> (e s) b n"))
         nc.sync.dma_start(dst_sb[:], dst)
@@ -104,10 +104,10 @@ def tile_moe_hie_none_kernel(
                 nc.vector.tensor_copy(words[:, s, :], xw[:, s, :].indirect(cols))
             planes = (both[min(f, 1)], second[min(f, 1)])
             start_col = max(f - 1, 0) * C1
-            for s in range(S):
-                w_words = wgw0[:, s, :] if f == 0 else wgw12[:, (f - 1) * S + s, :]
-                w_scales = wgs01[:, f * S + s, :] if f < 2 else wgs2[:, s, :]
-                for b in range(2):
+            for b in range(2):
+                for s in range(S):
+                    w_words = wgw0[:, s, :] if f == 0 else wgw12[:, (f - 1) * S + s, :]
+                    w_scales = wgs0[:, s, :] if f == 0 else wgs12[:, (f - 1) * S + s, :]
                     nc.tensor.matmul_mx(
                         out=a_banks[f][b][:],
                         lhsT=words[:, s, b * P:(b + 1) * P].bitcast(FP8X4),
@@ -204,9 +204,9 @@ def tile_moe_hie_none_kernel(
         res = [kept([P, T], F32, "res%d" % h) for h in range(2)]
         expert_layer(0, *quantised0)
         y0 = [results(0, h, "y0_%d" % h) for h in range(2)]
+        turn(2, last_rounded)
         expert_layer(1, *quantised1)
         upper1 = results(1, 0, "y1_0")
-        turn(2, last_rounded)
         for h in range(2):
             send_home(0, y0[h], res[h])
         send_home(1, upper1, res[0])

@@ -52,6 +52,7 @@ def tile_moe_hie_none_kernel(
         wes = kept([P, E, N], U8, "wes")
         gate_sb = kept([P, T], F32, "gate_sb")
         ident = kept([P, P], F32, "ident")
+        ident16 = kept([P, P], BF16, "ident16")
         zeros = kept([P, C1], F32, "zeros")
         pairs = keep.tile([P, BLOCKS * 2 * C1], BF16, name="pairs", tag="pairs", align_bytes=64)
         banks = [psum.tile([P, H], F32, name="bank%d" % b) for b in range(8)]
@@ -67,6 +68,7 @@ def tile_moe_hie_none_kernel(
         nc.gpsimd.memset(zeros[:], 0.0)
         nc.gpsimd.memset(wes[:].rearrange("p s t -> p (s t)").bitcast(I32), 0)
         make_identity(nc, ident[:])
+        make_identity(nc, ident16[:])
         pair_f32 = pairs[:].bitcast(F32)
         pair_u32 = pairs[:].bitcast(U32)
         nc.scalar.copy(pair_f32[:, PAD_BLOCK * C1:(PAD_BLOCK + 1) * C1], zeros[:])
@@ -118,16 +120,18 @@ def tile_moe_hie_none_kernel(
                         stop=(s == S - 1),
                     )
 
-        def round_out(f, tag):
-            rounded = keep.tile([P, 2 * H], BF16, name="aT%d" % f, tag=tag, align_bytes=64)
-            sorted_out = rounded[:].rearrange("m (b u p e) -> m b u p e", b=2, u=2, e=2)
-            sorted_in = [bank[:].rearrange("m (p u e) -> m u p e", u=2, e=2) for bank in a_banks[f]]
+        def round_out(f, run):
+            rounded = kept([P, 2 * H], BF16, "aT%d" % f)
+            sorted_out = rounded[:].rearrange("m (b u v p e) -> m b u v p e", b=2, u=2, v=2 // run, e=run)
+            sorted_in = [
+                bank[:].rearrange("m (p u v e) -> m u v p e", u=2, v=2 // run, e=run) for bank in a_banks[f]
+            ]
             nc.scalar.copy(sorted_out[:, 0], sorted_in[0])
             for u in range(2):
                 nc.scalar.copy(sorted_out[:, 1, u], sorted_in[1][:, u])
             return rounded
 
-        def turn(f, rounded):
+        def turn_pairs(f, rounded):
             for b in range(2):
                 for u in range(2):
                     nc.tensor.transpose(
@@ -137,13 +141,20 @@ def tile_moe_hie_none_kernel(
                     )
             for u in range(2):
                 first = HOME_BLOCK[f][u] * C1
-                if f < 2:
-                    nc.scalar.copy(pair_f32[:, first:first + C1], t_banks[u][:, 0:C1])
-                else:
-                    nc.scalar.copy(
-                        pairs[:, 2 * first:2 * (first + C1)].rearrange("p (e j) -> p e j", e=2),
-                        t_banks[u][:, 0:C1].bitcast(BF16).rearrange("p (j e) -> p e j", e=2),
+                nc.scalar.copy(pair_f32[:, first:first + C1], t_banks[u][:, 0:C1])
+
+        def turn_planes(f, rounded):
+            for b in range(2):
+                for t in range(4):
+                    column = (t % 2) * C1 + b * P
+                    nc.tensor.transpose(
+                        t_banks[t // 2][:].bitcast(BF16)[:, column:column + P],
+                        rounded[:, (4 * b + t) * P:(4 * b + t + 1) * P],
+                        ident16[:],
                     )
+            for u in range(2):
+                first = 2 * HOME_BLOCK[f][u] * C1
+                nc.scalar.copy(pairs[:, first:first + 2 * C1], t_banks[u][:].bitcast(BF16)[:, 0:2 * C1])
 
         def quantise(f):
             cols = offs2_sb[:, f * LC:(f + 1) * LC]
@@ -196,15 +207,15 @@ def tile_moe_hie_none_kernel(
         gather_scales(1)
         for f in range(2):
             group_layer(f)
-            turn(f, round_out(f, "aT%d" % f))
+            turn_pairs(f, round_out(f, 2))
         group_layer(2)
-        last_rounded = round_out(2, "aT2")
+        last_rounded = round_out(2, 1)
         quantised0 = quantise(0)
         quantised1 = quantise(1)
         res = [kept([P, T], F32, "res%d" % h) for h in range(2)]
         expert_layer(0, *quantised0)
         y0 = [results(0, h, "y0_%d" % h) for h in range(2)]
-        turn(2, last_rounded)
+        turn_planes(2, last_rounded)
         expert_layer(1, *quantised1)
         upper1 = results(1, 0, "y1_0")
         for h in range(2):

@@ -76,8 +76,8 @@ def tile_moe_hie_none_kernel(
         def load_scales(plane, rows):
             for q in range(4):
                 nc.sync.dma_start(
-                    plane[32 * q:32 * q + 4, :, :].bitcast(I32),
-                    rows[:, 4 * q:4 * q + 4, :].rearrange("c r w -> r c w").bitcast(I32),
+                    plane[q:P:32, :, :].bitcast(I32),
+                    rows[:, q:16:4, :].rearrange("c r w -> r c w").bitcast(I32),
                 )
 
         nc.sync.dma_start(offs_sb[:], offs)

@@ -156,22 +156,42 @@ def tile_moe_hie_none_kernel(
                 first = 2 * HOME_BLOCK[f][u] * C1
                 nc.scalar.copy(pairs[:, first:first + 2 * C1], t_banks[u][:].bitcast(BF16)[:, 0:2 * C1])
 
-        def quantise(f):
-            cols = offs2_sb[:, f * LC:(f + 1) * LC]
+        def window(f, u):
+            first = (HOME_BLOCK[f][u] - f) * C1
+            return pair_u32[:, first:first + 2 * C1].indirect(offs2_sb[:, f * LC:(f + 1) * LC])
+
+        def pick_woven(f):
             picked = kept([P, 4 * C1], BF16, "picked%d" % f)
-            picked_u32 = picked[:].bitcast(U32).rearrange("p (m u) -> p m u", u=2)
-            if f < 2:
-                for u in range(2):
-                    first = (HOME_BLOCK[f][u] - f) * C1
-                    nc.vector.tensor_copy(picked_u32[:, :, u], pair_u32[:, first:first + 2 * C1].indirect(cols))
-            else:
-                for t in range(4):
-                    first = (2 * HOME_BLOCK[f][0] + t - f) * C1
-                    nc.scalar.activation(
-                        picked[:].rearrange("p (m t) -> p m t", t=4)[:, :, t],
-                        pairs[:, first:first + T].indirect(cols),
-                        mybir.ActivationFunctionType.Copy,
-                    )
+            for u in range(2):
+                nc.vector.tensor_copy(picked[:].bitcast(U32).rearrange("p (m u) -> p m u", u=2)[:, :, u], window(f, u))
+            return picked
+
+        def pick_strips(f):
+            strips = kept([P, 2 * C1], U32, "strips%d" % f)
+            for u in range(2):
+                nc.vector.tensor_copy(strips[:, u * C1:(u + 1) * C1], window(f, u))
+            return strips
+
+        def weave(f, strips, tag):
+            picked = keep.tile([P, 4 * C1], BF16, name="picked%d" % f, tag=tag, align_bytes=64)
+            nc.scalar.copy(
+                picked[:].bitcast(U32).rearrange("p (m u) -> p m u", u=2),
+                strips[:].rearrange("p (u m) -> p m u", u=2),
+            )
+            return picked
+
+        def pick_planes(f):
+            picked = kept([P, 4 * C1], BF16, "picked%d" % f)
+            for t in range(4):
+                first = (2 * HOME_BLOCK[f][0] + t - f) * C1
+                nc.scalar.activation(
+                    picked[:].rearrange("p (m t) -> p m t", t=4)[:, :, t],
+                    pairs[:, first:first + T].indirect(offs2_sb[:, f * LC:(f + 1) * LC]),
+                    mybir.ActivationFunctionType.Copy,
+                )
+            return picked
+
+        def quantise(f, picked):
             codes = keep.tile([P, C1], U32, name="codes%d" % f, tag="codes%d" % f, align_bytes=64)
             scales = kept([P, C1], U8, "ascale%d" % f)
             nc.vector.quantize_mx(out=codes[:].bitcast(FP8X4), scales=scales[:], in_=picked[:])
@@ -210,18 +230,20 @@ def tile_moe_hie_none_kernel(
             turn_pairs(f, round_out(f, 2))
         group_layer(2)
         last_rounded = round_out(2, 1)
-        quantised0 = quantise(0)
-        quantised1 = quantise(1)
+        quantised0 = quantise(0, pick_woven(0))
+        strips1 = pick_strips(1)
         res = [kept([P, T], F32, "res%d" % h) for h in range(2)]
         expert_layer(0, *quantised0)
-        y0 = [results(0, h, "y0_%d" % h) for h in range(2)]
+        upper0 = results(0, 0, "y0_0")
+        picked1 = weave(1, strips1, "codes0")
+        lower0 = results(0, 1, "y0_1")
         turn_planes(2, last_rounded)
-        expert_layer(1, *quantised1)
+        send_home(0, upper0, res[0])
+        expert_layer(1, *quantise(1, picked1))
         upper1 = results(1, 0, "y1_0")
-        for h in range(2):
-            send_home(0, y0[h], res[h])
+        send_home(0, lower0, res[1])
         send_home(1, upper1, res[0])
-        expert_layer(2, *quantise(2))
+        expert_layer(2, *quantise(2, pick_planes(2)))
         send_home(1, results(1, 1, "pairs"), res[1])
         for h in range(2):
             send_home(2, results(2, h, "y2_%d" % h), res[h])

@@ -58,7 +58,7 @@ def tile_moe_hie_none_kernel(
         banks = [psum.tile([P, H], F32, name="bank%d" % b) for b in range(8)]
         a_banks = (banks[0:2], banks[2:4], banks[4:6])
         t_banks = banks[6:8]
-        y_banks = (t_banks, t_banks, a_banks[0])
+        y_banks = (t_banks, t_banks, a_banks[1])
 
         nc.gpsimd.memset(xs[:].bitcast(I32), 0)
         nc.vector.memset(wgs0[:].rearrange("p s t -> p (s t)").bitcast(I32), 0)
@@ -68,14 +68,14 @@ def tile_moe_hie_none_kernel(
         nc.gpsimd.memset(zeros[:], 0.0)
         nc.gpsimd.memset(wes[:].rearrange("p s t -> p (s t)").bitcast(I32), 0)
         make_identity(nc, ident[:])
-        make_identity(nc, ident16[:])
+        nc.vector.tensor_copy(ident16[:], ident[:])
         pair_f32 = pairs[:].bitcast(F32)
         pair_u32 = pairs[:].bitcast(U32)
         nc.scalar.copy(pair_f32[:, PAD_BLOCK * C1:(PAD_BLOCK + 1) * C1], zeros[:])
 
-        def load_scales(plane, rows):
+        def load_scales(plane, rows, queue):
             for q in range(4):
-                nc.sync.dma_start(
+                queue.dma_start(
                     plane[q:P:32, :, :].bitcast(I32),
                     rows[:, q:16:4, :].rearrange("c r w -> r c w").bitcast(I32),
                 )
@@ -85,12 +85,12 @@ def tile_moe_hie_none_kernel(
             nc.sync.dma_start(xs[32 * q:32 * q + 8, :].bitcast(I32), x_scales[:, 4 * q:4 * q + 4, :].bitcast(I32))
         nc.sync.dma_start(xw[:].bitcast(I32), x_words.rearrange("s p t d -> p s (t d)").bitcast(I32))
         nc.sync.dma_start(wgw0[:].bitcast(I32), wg_words[0].rearrange("s p w -> p s w").bitcast(I32))
-        load_scales(wgs0, wg_scales[0])
+        load_scales(wgs0, wg_scales[0], nc.sync)
         nc.sync.dma_start(wgw12[:].bitcast(I32), wg_words[1:3].rearrange("f s p w -> p (f s) w").bitcast(I32))
-        load_scales(wgs12, wg_scales[1:3].rearrange("f s b i -> (f s) b i"))
+        load_scales(wgs12, wg_scales[1:3].rearrange("f s b i -> (f s) b i"), nc.sync)
         nc.sync.dma_start(offs2_sb[:], offs2)
         nc.sync.dma_start(wew[:].bitcast(I32), we_words[:, 0].rearrange("e p n d -> p e (n d)").bitcast(I32))
-        load_scales(wes, we_scales.rearrange("e s b n -> (e s) b n"))
+        load_scales(wes, we_scales.rearrange("e s b n -> (e s) b n"), nc.gpsimd)
         nc.sync.dma_start(dst_sb[:], dst)
         nc.sync.dma_start(gate_sb[:], gate)
 
@@ -143,18 +143,18 @@ def tile_moe_hie_none_kernel(
                 first = HOME_BLOCK[f][u] * C1
                 nc.scalar.copy(pair_f32[:, first:first + C1], t_banks[u][:, 0:C1])
 
-        def turn_planes(f, rounded):
+        def turn_planes(f, rounded, into):
             for b in range(2):
                 for t in range(4):
                     column = (t % 2) * C1 + b * P
                     nc.tensor.transpose(
-                        t_banks[t // 2][:].bitcast(BF16)[:, column:column + P],
+                        into[t // 2][:].bitcast(BF16)[:, column:column + P],
                         rounded[:, (4 * b + t) * P:(4 * b + t + 1) * P],
                         ident16[:],
                     )
             for u in range(2):
                 first = 2 * HOME_BLOCK[f][u] * C1
-                nc.scalar.copy(pairs[:, first:first + 2 * C1], t_banks[u][:].bitcast(BF16)[:, 0:2 * C1])
+                nc.scalar.copy(pairs[:, first:first + 2 * C1], into[u][:].bitcast(BF16)[:, 0:2 * C1])
 
         def window(f, u):
             first = (HOME_BLOCK[f][u] - f) * C1
@@ -167,7 +167,8 @@ def tile_moe_hie_none_kernel(
             return picked
 
         def pick_strips(f):
-            strips = kept([P, 2 * C1], U32, "strips%d" % f)
+            first = HOME_BLOCK[f + 1][0] * C1
+            strips = pair_u32[:, first:first + 2 * C1]
             for u in range(2):
                 nc.vector.tensor_copy(strips[:, u * C1:(u + 1) * C1], window(f, u))
             return strips
@@ -176,36 +177,37 @@ def tile_moe_hie_none_kernel(
             picked = keep.tile([P, 4 * C1], BF16, name="picked%d" % f, tag=tag, align_bytes=64)
             nc.scalar.copy(
                 picked[:].bitcast(U32).rearrange("p (m u) -> p m u", u=2),
-                strips[:].rearrange("p (u m) -> p m u", u=2),
+                strips.rearrange("p (u m) -> p m u", u=2),
             )
             return picked
 
-        def pick_planes(f):
-            picked = kept([P, 4 * C1], BF16, "picked%d" % f)
+        def pick_planes(f, e, tag):
+            picked = keep.tile([P, 4 * C2], BF16, name="picked_e%d" % e, tag=tag, align_bytes=64)
             for t in range(4):
                 first = (2 * HOME_BLOCK[f][0] + t - f) * C1
                 nc.scalar.activation(
                     picked[:].rearrange("p (m t) -> p m t", t=4)[:, :, t],
-                    pairs[:, first:first + T].indirect(offs2_sb[:, f * LC:(f + 1) * LC]),
+                    pairs[:, first:first + T].indirect(offs2_sb[:, e * C2 // 16:(e + 1) * C2 // 16]),
                     mybir.ActivationFunctionType.Copy,
                 )
             return picked
 
-        def quantise(f, picked):
-            codes = keep.tile([P, C1], U32, name="codes%d" % f, tag="codes%d" % f, align_bytes=64)
-            scales = kept([P, C1], U8, "ascale%d" % f)
+        def quantise(name, picked, columns):
+            tag = "y0_1" if name == "4" else "codes" + name
+            codes = keep.tile([P, columns], U32, name="codes" + name, tag=tag, align_bytes=64)
+            scales = kept([P, columns], U8, "ascale" + name)
             nc.vector.quantize_mx(out=codes[:].bitcast(FP8X4), scales=scales[:], in_=picked[:])
-            return codes, scales
+            return [(codes[:, c:c + C2], scales[:, c:c + C2]) for c in range(0, columns, C2)]
 
-        def expert_layer(f, codes, scales):
+        def expert_layer(f, operands):
             for h in range(2):
-                for e in range(2):
+                for e, (codes, scales) in enumerate(operands):
                     nc.tensor.matmul_mx(
                         out=y_banks[f][h][:, e * C2:(e + 1) * C2],
                         lhsT=wew[:, 2 * f + e, h * P:(h + 1) * P].bitcast(FP8X4),
                         lhsT_scale=wes[:, 2 * f + e, h * P:(h + 1) * P],
-                        rhs=codes[:, e * C2:(e + 1) * C2].bitcast(FP8X4),
-                        rhs_scale=scales[:, e * C2:(e + 1) * C2],
+                        rhs=codes.bitcast(FP8X4),
+                        rhs_scale=scales,
                         start=True,
                         stop=True,
                     )
@@ -230,20 +232,23 @@ def tile_moe_hie_none_kernel(
             turn_pairs(f, round_out(f, 2))
         group_layer(2)
         last_rounded = round_out(2, 1)
-        quantised0 = quantise(0, pick_woven(0))
+        quantised0 = quantise("0", pick_woven(0), C1)
         strips1 = pick_strips(1)
         res = [kept([P, T], F32, "res%d" % h) for h in range(2)]
-        expert_layer(0, *quantised0)
+        expert_layer(0, quantised0)
         upper0 = results(0, 0, "y0_0")
         picked1 = weave(1, strips1, "codes0")
         lower0 = results(0, 1, "y0_1")
-        turn_planes(2, last_rounded)
+        turn_planes(2, last_rounded, a_banks[0])
         send_home(0, upper0, res[0])
-        expert_layer(1, *quantise(1, picked1))
+        quantised1 = quantise("1", picked1, C1)
+        picked4 = pick_planes(2, 4, "picked_e4")
+        expert_layer(1, quantised1)
         upper1 = results(1, 0, "y1_0")
         send_home(0, lower0, res[1])
         send_home(1, upper1, res[0])
-        expert_layer(2, *quantise(2, pick_planes(2)))
+        picked5 = pick_planes(2, 5, "codes1")
+        expert_layer(2, quantise("4", picked4, C2) + quantise("5", picked5, C2))
         send_home(1, results(1, 1, "pairs"), res[1])
         for h in range(2):
             send_home(2, results(2, h, "y2_%d" % h), res[h])

@@ -82,7 +82,9 @@ def tile_moe_hie_none_kernel(
 
         nc.sync.dma_start(offs_sb[:], offs)
         for q in range(4):
-            nc.sync.dma_start(xs[32 * q:32 * q + 8, :].bitcast(I32), x_scales[:, 4 * q:4 * q + 4, :].bitcast(I32))
+            nc.sync.dma_start(
+                xs[q:P:16, :].bitcast(I32), x_scales.rearrange("s (c r) t -> r c s t", r=4)[q].bitcast(I32)
+            )
         nc.sync.dma_start(xw[:].bitcast(I32), x_words.rearrange("s p t d -> p s (t d)").bitcast(I32))
         nc.sync.dma_start(wgw0[:].bitcast(I32), wg_words[0].rearrange("s p w -> p s w").bitcast(I32))
         load_scales(wgs0, wg_scales[0], nc.sync)
@@ -97,7 +99,7 @@ def tile_moe_hie_none_kernel(
         def gather_scales(i):
             lo, hi = spans[i]
             nc.vector.tensor_copy(both[i][:], xs[:].indirect(offs_sb[:, lo // 16:hi // 16]))
-            nc.scalar.dma_start(second[i][0:112, :].bitcast(I32), both[i][4:116, :].bitcast(I32))
+            nc.scalar.dma_start(second[i][0:112, :].bitcast(I32), both[i][16:128, :].bitcast(I32))
 
         def group_layer(f):
             cols = offs_sb[:, f * LC:(f + 1) * LC]
@@ -192,8 +194,7 @@ def tile_moe_hie_none_kernel(
                 )
             return picked
 
-        def quantise(name, picked, columns):
-            tag = "y0_1" if name == "4" else "codes" + name
+        def quantise(name, picked, columns, tag):
             codes = keep.tile([P, columns], U32, name="codes" + name, tag=tag, align_bytes=64)
             scales = kept([P, columns], U8, "ascale" + name)
             nc.vector.quantize_mx(out=codes[:].bitcast(FP8X4), scales=scales[:], in_=picked[:])
@@ -217,6 +218,23 @@ def tile_moe_hie_none_kernel(
             nc.scalar.copy(y[:], y_banks[f][h][:, 0:C1])
             return y
 
+        def lone_expert(e, operand):
+            codes, scales = operand
+            bank = y_banks[2][e % 2]
+            for h in range(2):
+                nc.tensor.matmul_mx(
+                    out=bank[:, h * C2:(h + 1) * C2],
+                    lhsT=wew[:, e, h * P:(h + 1) * P].bitcast(FP8X4),
+                    lhsT_scale=wes[:, e, h * P:(h + 1) * P],
+                    rhs=codes.bitcast(FP8X4),
+                    rhs_scale=scales,
+                    start=True,
+                    stop=True,
+                )
+            y = kept([P, 2 * C2], F32, "y_e%d" % e)
+            nc.scalar.copy(y[:], bank[:, 0:2 * C2])
+            return y
+
         def send_home(f, y, home):
             nc.vector.tensor_tensor(
                 home[:].indirect(dst_sb[:, f * LC:(f + 1) * LC]),
@@ -232,7 +250,7 @@ def tile_moe_hie_none_kernel(
             turn_pairs(f, round_out(f, 2))
         group_layer(2)
         last_rounded = round_out(2, 1)
-        quantised0 = quantise("0", pick_woven(0), C1)
+        quantised0 = quantise("0", pick_woven(0), C1, "codes0")
         strips1 = pick_strips(1)
         res = [kept([P, T], F32, "res%d" % h) for h in range(2)]
         expert_layer(0, quantised0)
@@ -241,16 +259,25 @@ def tile_moe_hie_none_kernel(
         lower0 = results(0, 1, "y0_1")
         turn_planes(2, last_rounded, a_banks[0])
         send_home(0, upper0, res[0])
-        quantised1 = quantise("1", picked1, C1)
+        quantised1 = quantise("1", picked1, C1, "codes1")
         picked4 = pick_planes(2, 4, "picked_e4")
         expert_layer(1, quantised1)
         upper1 = results(1, 0, "y1_0")
         send_home(0, lower0, res[1])
         send_home(1, upper1, res[0])
+        lower1 = results(1, 1, "y1_1")
         picked5 = pick_planes(2, 5, "codes1")
-        expert_layer(2, quantise("4", picked4, C2) + quantise("5", picked5, C2))
-        send_home(1, results(1, 1, "pairs"), res[1])
-        for h in range(2):
-            send_home(2, results(2, h, "y2_%d" % h), res[h])
+        last = [lone_expert(4, quantise("4", picked4, C2, "y0_1")[0])]
+        send_home(1, lower1, res[1])
+        last.append(lone_expert(5, quantise("5", picked5, C2, "y1_0")[0]))
+        for e in range(2):
+            lo = (4 + e) * C2
+            for h in range(2):
+                nc.vector.tensor_tensor(
+                    res[h][:].indirect(dst_sb[:, lo // 16:(lo + C2) // 16]),
+                    last[e][:, h * C2:(h + 1) * C2],
+                    gate_sb[:, lo:lo + C2],
+                    mult,
+                )
         for h in range(2):
             nc.sync.dma_start(out[h * P:(h + 1) * P, :], res[h][:])

@@ -53,12 +53,12 @@ def tile_moe_hie_none_kernel(
         gate_sb = kept([P, T], F32, "gate_sb")
         ident = kept([P, P], F32, "ident")
         ident16 = kept([P, P], BF16, "ident16")
-        zeros = kept([P, C1], F32, "zeros")
+        zeros = kept([P, 2 * C1], F32, "zeros")
         pairs = keep.tile([P, BLOCKS * 2 * C1], BF16, name="pairs", tag="pairs", align_bytes=64)
         banks = [psum.tile([P, H], F32, name="bank%d" % b) for b in range(8)]
         a_banks = (banks[0:2], banks[2:4], banks[4:6])
         t_banks = banks[6:8]
-        y_banks = (t_banks, t_banks, a_banks[1])
+        y_banks = ((a_banks[1][0], t_banks[1]), t_banks, a_banks[2])
 
         nc.gpsimd.memset(xs[:].bitcast(I32), 0)
         nc.vector.memset(wgs0[:].rearrange("p s t -> p (s t)").bitcast(I32), 0)
@@ -68,10 +68,9 @@ def tile_moe_hie_none_kernel(
         nc.gpsimd.memset(zeros[:], 0.0)
         nc.gpsimd.memset(wes[:].rearrange("p s t -> p (s t)").bitcast(I32), 0)
         make_identity(nc, ident[:])
-        nc.vector.tensor_copy(ident16[:], ident[:])
         pair_f32 = pairs[:].bitcast(F32)
         pair_u32 = pairs[:].bitcast(U32)
-        nc.scalar.copy(pair_f32[:, PAD_BLOCK * C1:(PAD_BLOCK + 1) * C1], zeros[:])
+        nc.scalar.copy(pair_f32[:, PAD_BLOCK * C1:(PAD_BLOCK + 1) * C1], zeros[:, 0:C1])
 
         def load_scales(plane, rows, queue):
             for q in range(4):
@@ -93,6 +92,7 @@ def tile_moe_hie_none_kernel(
         nc.sync.dma_start(offs2_sb[:], offs2)
         nc.sync.dma_start(wew[:].bitcast(I32), we_words[:, 0].rearrange("e p n d -> p e (n d)").bitcast(I32))
         load_scales(wes, we_scales.rearrange("e s b n -> (e s) b n"), nc.gpsimd)
+        make_identity(nc, ident16[:])
         nc.sync.dma_start(dst_sb[:], dst)
         nc.sync.dma_start(gate_sb[:], gate)
 
@@ -101,11 +101,14 @@ def tile_moe_hie_none_kernel(
             nc.vector.tensor_copy(both[i][:], xs[:].indirect(offs_sb[:, lo // 16:hi // 16]))
             nc.scalar.dma_start(second[i][0:112, :].bitcast(I32), both[i][16:128, :].bitcast(I32))
 
-        def group_layer(f):
-            cols = offs_sb[:, f * LC:(f + 1) * LC]
-            words = kept([P, S, C1], U32, "gw%d" % f)
+        def gather_words(i):
+            lo, hi = spans[i]
+            words = kept([P, S, hi - lo], U32, "gw%d" % lo)
             for s in range(S):
-                nc.vector.tensor_copy(words[:, s, :], xw[:, s, :].indirect(cols))
+                nc.vector.tensor_copy(words[:, s, :], xw[:, s, :].indirect(offs_sb[:, lo // 16:hi // 16]))
+            return words
+
+        def group_layer(f, words):
             planes = (both[min(f, 1)], second[min(f, 1)])
             start_col = max(f - 1, 0) * C1
             for b in range(2):
@@ -114,7 +117,7 @@ def tile_moe_hie_none_kernel(
                     w_scales = wgs0[:, s, :] if f == 0 else wgs12[:, (f - 1) * S + s, :]
                     nc.tensor.matmul_mx(
                         out=a_banks[f][b][:],
-                        lhsT=words[:, s, b * P:(b + 1) * P].bitcast(FP8X4),
+                        lhsT=words[:, s, start_col + b * P:start_col + (b + 1) * P].bitcast(FP8X4),
                         lhsT_scale=planes[s][:, start_col + b * P:start_col + (b + 1) * P],
                         rhs=w_words.bitcast(FP4X4),
                         rhs_scale=w_scales,
@@ -123,7 +126,7 @@ def tile_moe_hie_none_kernel(
                     )
 
         def round_out(f, run):
-            rounded = kept([P, 2 * H], BF16, "aT%d" % f)
+            rounded = keep.tile([P, 2 * H], BF16, name="aT%d" % f, tag="aT%d" % f, align_bytes=64)
             sorted_out = rounded[:].rearrange("m (b u v p e) -> m b u v p e", b=2, u=2, v=2 // run, e=run)
             sorted_in = [
                 bank[:].rearrange("m (p u v e) -> m u v p e", u=2, v=2 // run, e=run) for bank in a_banks[f]
@@ -245,16 +248,31 @@ def tile_moe_hie_none_kernel(
 
         gather_scales(0)
         gather_scales(1)
-        for f in range(2):
-            group_layer(f)
-            turn_pairs(f, round_out(f, 2))
-        group_layer(2)
+        warm_codes = kept([P, C1], U32, "warm_codes")
+        warm_scales = kept([P, C1], U8, "warm_scales")
+        nc.vector.quantize_mx(out=warm_codes[:].bitcast(FP8X4), scales=warm_scales[:], in_=zeros[:].bitcast(BF16))
+        for bank in t_banks:
+            nc.tensor.matmul_mx(
+                out=bank[:, 0:C1],
+                lhsT=warm_codes[:, 0:P].bitcast(FP8X4),
+                lhsT_scale=both[1][:, 0:P],
+                rhs=warm_codes[:].bitcast(FP8X4),
+                rhs_scale=warm_scales[:],
+                start=True,
+                stop=True,
+            )
+        group_layer(0, gather_words(0))
+        turn_pairs(0, round_out(0, 2))
+        later_words = gather_words(1)
+        group_layer(1, later_words)
+        turn_pairs(1, round_out(1, 2))
+        group_layer(2, later_words)
         last_rounded = round_out(2, 1)
         quantised0 = quantise("0", pick_woven(0), C1, "codes0")
         strips1 = pick_strips(1)
         res = [kept([P, T], F32, "res%d" % h) for h in range(2)]
         expert_layer(0, quantised0)
-        upper0 = results(0, 0, "y0_0")
+        upper0 = results(0, 0, "aT1")
         picked1 = weave(1, strips1, "codes0")
         lower0 = results(0, 1, "y0_1")
         turn_planes(2, last_rounded, a_banks[0])

@@ -146,7 +146,8 @@ def tile_moe_hie_none_kernel(
                     )
             for u in range(2):
                 first = HOME_BLOCK[f][u] * C1
-                nc.scalar.copy(pair_f32[:, first:first + C1], t_banks[u][:, 0:C1])
+                move = nc.vector.tensor_copy if (f, u) == (0, 0) else nc.scalar.copy
+                move(pair_f32[:, first:first + C1], t_banks[u][:, 0:C1])
 
         def turn_planes(f, rounded, into):
             for b in range(2):

@@ -53,7 +53,7 @@ def tile_moe_hie_none_kernel(
         gate_sb = kept([P, T], F32, "gate_sb")
         ident = kept([P, P], F32, "ident")
         ident16 = kept([P, P], BF16, "ident16")
-        zeros = kept([P, 2 * C1], F32, "zeros")
+        zeros = kept([P, C1], F32, "zeros")
         pairs = keep.tile([P, BLOCKS * 2 * C1], BF16, name="pairs", tag="pairs", align_bytes=64)
         banks = [psum.tile([P, H], F32, name="bank%d" % b) for b in range(8)]
         a_banks = (banks[0:2], banks[2:4], banks[4:6])
@@ -70,7 +70,7 @@ def tile_moe_hie_none_kernel(
         make_identity(nc, ident[:])
         pair_f32 = pairs[:].bitcast(F32)
         pair_u32 = pairs[:].bitcast(U32)
-        nc.scalar.copy(pair_f32[:, PAD_BLOCK * C1:(PAD_BLOCK + 1) * C1], zeros[:, 0:C1])
+        nc.scalar.copy(pair_f32[:, PAD_BLOCK * C1:(PAD_BLOCK + 1) * C1], zeros[:])
 
         def load_scales(plane, rows, queue):
             for q in range(4):
@@ -249,19 +249,6 @@ def tile_moe_hie_none_kernel(
 
         gather_scales(0)
         gather_scales(1)
-        warm_codes = kept([P, C1], U32, "warm_codes")
-        warm_scales = kept([P, C1], U8, "warm_scales")
-        nc.vector.quantize_mx(out=warm_codes[:].bitcast(FP8X4), scales=warm_scales[:], in_=zeros[:].bitcast(BF16))
-        for bank in t_banks:
-            nc.tensor.matmul_mx(
-                out=bank[:, 0:C1],
-                lhsT=warm_codes[:, 0:P].bitcast(FP8X4),
-                lhsT_scale=both[1][:, 0:P],
-                rhs=warm_codes[:].bitcast(FP8X4),
-                rhs_scale=warm_scales[:],
-                start=True,
-                stop=True,
-            )
         group_layer(0, gather_words(0))
         turn_pairs(0, round_out(0, 2))
         later_words = gather_words(1)

@@ -21,6 +21,7 @@ LC = C1 // 16
 HOME_BLOCK = ((1, 0), (3, 4), (5, 6))
 PAD_BLOCK = 2
 BLOCKS = 7
+ODD_WORDS = T // 8 - 1
 
 
 def tile_moe_hie_none_kernel(
@@ -60,7 +61,8 @@ def tile_moe_hie_none_kernel(
         t_banks = banks[6:8]
         y_banks = ((a_banks[1][0], t_banks[1]), t_banks, a_banks[2])
 
-        nc.gpsimd.memset(xs[:].bitcast(I32), 0)
+        for lo, hi in ((0, ODD_WORDS), (ODD_WORDS, T // 4)):
+            nc.vector.memset(xs[:].bitcast(I32)[:, lo:hi], 0)
         nc.vector.memset(wgs0[:].rearrange("p s t -> p (s t)").bitcast(I32), 0)
         for plane in second:
             nc.vector.memset(plane[:].bitcast(I32), 0)

@@ -148,8 +148,7 @@ def tile_moe_hie_none_kernel(
                     )
             for u in range(2):
                 first = HOME_BLOCK[f][u] * C1
-                move = nc.vector.tensor_copy if (f, u) == (0, 0) else nc.scalar.copy
-                move(pair_f32[:, first:first + C1], t_banks[u][:, 0:C1])
+                nc.scalar.copy(pair_f32[:, first:first + C1], t_banks[u][:, 0:C1])
 
         def turn_planes(f, rounded, into):
             for b in range(2):

from contextlib import ExitStack

import concourse.mybir as mybir
from concourse.masks import make_identity

K, T, G, C1, E, C2, H, N = 1024, 768, 3, 256, 6, 128, 512, 256
FLOPS = 2 * T * (K * H + H * N)

F32 = mybir.dt.float32
BF16 = mybir.dt.bfloat16
I32 = mybir.dt.int32
U32 = mybir.dt.uint32
U16 = mybir.dt.uint16
U8 = mybir.dt.uint8
FP8X4 = mybir.dt.float8_e4m3fn_x4
FP4X4 = mybir.dt.float4_e2m1fn_x4

P = 128
S = K // 512
LC = C1 // 16
HOME_BLOCK = ((1, 0), (3, 4), (5, 6))
PAD_BLOCK = 2
BLOCKS = 7
ODD_WORDS = T // 8 - 1


def tile_moe_hie_none_kernel(
    tc, x_words, x_scales, wg_words, wg_scales, we_words, we_scales, gate, offs, offs2, dst, out
):
    nc = tc.nc
    mult = mybir.AluOpType.mult

    with ExitStack() as ctx:
        keep = ctx.enter_context(tc.tile_pool(name="keep", bufs=1))
        psum = ctx.enter_context(tc.psum_pool(name="psum", bufs=1))

        def kept(shape, dtype, name):
            return keep.tile(shape, dtype, name=name, align_bytes=64)

        offs_sb = kept([P, T // 16], U16, "offs_sb")
        offs2_sb = kept([P, T // 16], U16, "offs2_sb")
        dst_sb = kept([P, T // 16], U16, "dst_sb")
        xw = kept([P, S, T], U32, "xw")
        xs = kept([P, T], U8, "xs")
        wgw0 = kept([P, S, 2 * H], U8, "wgw0")
        wgw12 = kept([P, 2 * S, 2 * H], U8, "wgw12")
        wgs0 = kept([P, S, H], U8, "wgs0")
        wgs12 = kept([P, 2 * S, H], U8, "wgs12")
        wew = kept([P, E, N], U32, "wew")
        spans = ((0, C1), (C1, T))
        both = [kept([P, hi - lo], U8, "both%d" % lo) for lo, hi in spans]
        second = [kept([P, hi - lo], U8, "second%d" % lo) for lo, hi in spans]
        wes = kept([P, E, N], U8, "wes")
        gate_sb = kept([P, T], F32, "gate_sb")
        ident = kept([P, P], F32, "ident")
        ident16 = kept([P, P], BF16, "ident16")
        zeros = kept([P, C1], F32, "zeros")
        pairs = keep.tile([P, BLOCKS * 2 * C1], BF16, name="pairs", tag="pairs", align_bytes=64)
        banks = [psum.tile([P, H], F32, name="bank%d" % b) for b in range(8)]
        a_banks = (banks[0:2], banks[2:4], banks[4:6])
        t_banks = banks[6:8]
        y_banks = ((a_banks[1][0], t_banks[1]), t_banks, a_banks[2])

        for lo, hi in ((0, ODD_WORDS), (ODD_WORDS, T // 4)):
            nc.vector.memset(xs[:].bitcast(I32)[:, lo:hi], 0)
        nc.vector.memset(wgs0[:].rearrange("p s t -> p (s t)").bitcast(I32), 0)
        for plane in second:
            nc.vector.memset(plane[:].bitcast(I32), 0)
        nc.vector.memset(wgs12[:].rearrange("p s t -> p (s t)").bitcast(I32), 0)
        nc.gpsimd.memset(zeros[:], 0.0)
        nc.gpsimd.memset(wes[:].rearrange("p s t -> p (s t)").bitcast(I32), 0)
        make_identity(nc, ident[:])
        pair_f32 = pairs[:].bitcast(F32)
        pair_u32 = pairs[:].bitcast(U32)
        nc.scalar.copy(pair_f32[:, PAD_BLOCK * C1:(PAD_BLOCK + 1) * C1], zeros[:])

        def load_scales(plane, rows, queue):
            for q in range(4):
                queue.dma_start(
                    plane[q:P:32, :, :].bitcast(I32),
                    rows[:, q:16:4, :].rearrange("c r w -> r c w").bitcast(I32),
                )

        nc.sync.dma_start(offs_sb[:], offs)
        for q in range(4):
            nc.sync.dma_start(
                xs[q:P:16, :].bitcast(I32), x_scales.rearrange("s (c r) t -> r c s t", r=4)[q].bitcast(I32)
            )
        nc.sync.dma_start(xw[:].bitcast(I32), x_words.rearrange("s p t d -> p s (t d)").bitcast(I32))
        nc.sync.dma_start(wgw0[:].bitcast(I32), wg_words[0].rearrange("s p w -> p s w").bitcast(I32))
        load_scales(wgs0, wg_scales[0], nc.sync)
        nc.sync.dma_start(wgw12[:].bitcast(I32), wg_words[1:3].rearrange("f s p w -> p (f s) w").bitcast(I32))
        load_scales(wgs12, wg_scales[1:3].rearrange("f s b i -> (f s) b i"), nc.sync)
        nc.sync.dma_start(offs2_sb[:], offs2)
        nc.sync.dma_start(wew[:].bitcast(I32), we_words[:, 0].rearrange("e p n d -> p e (n d)").bitcast(I32))
        load_scales(wes, we_scales.rearrange("e s b n -> (e s) b n"), nc.gpsimd)
        make_identity(nc, ident16[:])
        nc.sync.dma_start(dst_sb[:], dst)
        nc.sync.dma_start(gate_sb[:], gate)

        def gather_scales(i):
            lo, hi = spans[i]
            nc.vector.tensor_copy(both[i][:], xs[:].indirect(offs_sb[:, lo // 16:hi // 16]))
            nc.scalar.dma_start(second[i][0:112, :].bitcast(I32), both[i][16:128, :].bitcast(I32))

        def gather_words(i):
            lo, hi = spans[i]
            words = kept([P, S, hi - lo], U32, "gw%d" % lo)
            for s in range(S):
                nc.vector.tensor_copy(words[:, s, :], xw[:, s, :].indirect(offs_sb[:, lo // 16:hi // 16]))
            return words

        def group_layer(f, words):
            planes = (both[min(f, 1)], second[min(f, 1)])
            start_col = max(f - 1, 0) * C1
            for b in range(2):
                for s in range(S):
                    w_words = wgw0[:, s, :] if f == 0 else wgw12[:, (f - 1) * S + s, :]
                    w_scales = wgs0[:, s, :] if f == 0 else wgs12[:, (f - 1) * S + s, :]
                    nc.tensor.matmul_mx(
                        out=a_banks[f][b][:],
                        lhsT=words[:, s, start_col + b * P:start_col + (b + 1) * P].bitcast(FP8X4),
                        lhsT_scale=planes[s][:, start_col + b * P:start_col + (b + 1) * P],
                        rhs=w_words.bitcast(FP4X4),
                        rhs_scale=w_scales,
                        start=(s == 0),
                        stop=(s == S - 1),
                    )

        def round_out(f, run):
            rounded = keep.tile([P, 2 * H], BF16, name="aT%d" % f, tag="aT%d" % f, align_bytes=64)
            sorted_out = rounded[:].rearrange("m (b u v p e) -> m b u v p e", b=2, u=2, v=2 // run, e=run)
            sorted_in = [
                bank[:].rearrange("m (p u v e) -> m u v p e", u=2, v=2 // run, e=run) for bank in a_banks[f]
            ]
            nc.scalar.copy(sorted_out[:, 0], sorted_in[0])
            for u in range(2):
                nc.scalar.copy(sorted_out[:, 1, u], sorted_in[1][:, u])
            return rounded

        def turn_pairs(f, rounded):
            for b in range(2):
                for u in range(2):
                    nc.tensor.transpose(
                        t_banks[u][:, b * P:(b + 1) * P],
                        rounded[:].bitcast(F32)[:, (2 * b + u) * P:(2 * b + u + 1) * P],
                        ident[:],
                    )
            for u in range(2):
                first = HOME_BLOCK[f][u] * C1
                nc.scalar.copy(pair_f32[:, first:first + C1], t_banks[u][:, 0:C1])

        def turn_planes(f, rounded, into):
            for b in range(2):
                for t in range(4):
                    column = (t % 2) * C1 + b * P
                    nc.tensor.transpose(
                        into[t // 2][:].bitcast(BF16)[:, column:column + P],
                        rounded[:, (4 * b + t) * P:(4 * b + t + 1) * P],
                        ident16[:],
                    )
            for u in range(2):
                first = 2 * HOME_BLOCK[f][u] * C1
                nc.scalar.copy(pairs[:, first:first + 2 * C1], into[u][:].bitcast(BF16)[:, 0:2 * C1])

        def window(f, u):
            first = (HOME_BLOCK[f][u] - f) * C1
            return pair_u32[:, first:first + 2 * C1].indirect(offs2_sb[:, f * LC:(f + 1) * LC])

        def pick_woven(f):
            picked = kept([P, 4 * C1], BF16, "picked%d" % f)
            for u in range(2):
                nc.vector.tensor_copy(picked[:].bitcast(U32).rearrange("p (m u) -> p m u", u=2)[:, :, u], window(f, u))
            return picked

        def pick_strips(f):
            first = HOME_BLOCK[f + 1][0] * C1
            strips = pair_u32[:, first:first + 2 * C1]
            for u in range(2):
                nc.vector.tensor_copy(strips[:, u * C1:(u + 1) * C1], window(f, u))
            return strips

        def weave(f, strips, tag):
            picked = keep.tile([P, 4 * C1], BF16, name="picked%d" % f, tag=tag, align_bytes=64)
            nc.scalar.copy(
                picked[:].bitcast(U32).rearrange("p (m u) -> p m u", u=2),
                strips.rearrange("p (u m) -> p m u", u=2),
            )
            return picked

        def pick_planes(f, e, tag):
            picked = keep.tile([P, 4 * C2], BF16, name="picked_e%d" % e, tag=tag, align_bytes=64)
            for t in range(4):
                first = (2 * HOME_BLOCK[f][0] + t - f) * C1
                nc.scalar.activation(
                    picked[:].rearrange("p (m t) -> p m t", t=4)[:, :, t],
                    pairs[:, first:first + T].indirect(offs2_sb[:, e * C2 // 16:(e + 1) * C2 // 16]),
                    mybir.ActivationFunctionType.Copy,
                )
            return picked

        def quantise(name, picked, columns, tag):
            codes = keep.tile([P, columns], U32, name="codes" + name, tag=tag, align_bytes=64)
            scales = kept([P, columns], U8, "ascale" + name)
            nc.vector.quantize_mx(out=codes[:].bitcast(FP8X4), scales=scales[:], in_=picked[:])
            return [(codes[:, c:c + C2], scales[:, c:c + C2]) for c in range(0, columns, C2)]

        def expert_layer(f, operands):
            for h in range(2):
                for e, (codes, scales) in enumerate(operands):
                    nc.tensor.matmul_mx(
                        out=y_banks[f][h][:, e * C2:(e + 1) * C2],
                        lhsT=wew[:, 2 * f + e, h * P:(h + 1) * P].bitcast(FP8X4),
                        lhsT_scale=wes[:, 2 * f + e, h * P:(h + 1) * P],
                        rhs=codes.bitcast(FP8X4),
                        rhs_scale=scales,
                        start=True,
                        stop=True,
                    )

        def results(f, h, tag):
            y = keep.tile([P, C1], F32, name="y%d_%d" % (f, h), tag=tag, align_bytes=64)
            nc.scalar.copy(y[:], y_banks[f][h][:, 0:C1])
            return y

        def lone_expert(e, operand):
            codes, scales = operand
            bank = y_banks[2][e % 2]
            for h in range(2):
                nc.tensor.matmul_mx(
                    out=bank[:, h * C2:(h + 1) * C2],
                    lhsT=wew[:, e, h * P:(h + 1) * P].bitcast(FP8X4),
                    lhsT_scale=wes[:, e, h * P:(h + 1) * P],
                    rhs=codes.bitcast(FP8X4),
                    rhs_scale=scales,
                    start=True,
                    stop=True,
                )
            y = kept([P, 2 * C2], F32, "y_e%d" % e)
            nc.scalar.copy(y[:], bank[:, 0:2 * C2])
            return y

        def send_home(f, y, home):
            nc.vector.tensor_tensor(
                home[:].indirect(dst_sb[:, f * LC:(f + 1) * LC]),
                y[:],
                gate_sb[:, f * C1:(f + 1) * C1],
                mult,
            )

        gather_scales(0)
        gather_scales(1)
        group_layer(0, gather_words(0))
        turn_pairs(0, round_out(0, 2))
        later_words = gather_words(1)
        group_layer(1, later_words)
        turn_pairs(1, round_out(1, 2))
        group_layer(2, later_words)
        last_rounded = round_out(2, 1)
        quantised0 = quantise("0", pick_woven(0), C1, "codes0")
        strips1 = pick_strips(1)
        res = [kept([P, T], F32, "res%d" % h) for h in range(2)]
        expert_layer(0, quantised0)
        upper0 = results(0, 0, "aT1")
        picked1 = weave(1, strips1, "codes0")
        lower0 = results(0, 1, "y0_1")
        turn_planes(2, last_rounded, a_banks[0])
        send_home(0, upper0, res[0])
        quantised1 = quantise("1", picked1, C1, "codes1")
        picked4 = pick_planes(2, 4, "picked_e4")
        expert_layer(1, quantised1)
        upper1 = results(1, 0, "y1_0")
        send_home(0, lower0, res[1])
        send_home(1, upper1, res[0])
        lower1 = results(1, 1, "y1_1")
        picked5 = pick_planes(2, 5, "codes1")
        last = [lone_expert(4, quantise("4", picked4, C2, "y0_1")[0])]
        send_home(1, lower1, res[1])
        last.append(lone_expert(5, quantise("5", picked5, C2, "y1_0")[0]))
        for e in range(2):
            lo = (4 + e) * C2
            for h in range(2):
                nc.vector.tensor_tensor(
                    res[h][:].indirect(dst_sb[:, lo // 16:(lo + C2) // 16]),
                    last[e][:, h * C2:(h + 1) * C2],
                    gate_sb[:, lo:lo + C2],
                    mult,
                )
        for h in range(2):
            nc.sync.dma_start(out[h * P:(h + 1) * P, :], res[h][:])
